import numpy as np
import ml_dtypes


def mxq(x, axis, fmt="e4m3"):
    dtype, down = {"e4m3": (ml_dtypes.float8_e4m3fn, 7), "e5m2": (ml_dtypes.float8_e5m2, 14)}[fmt]
    v = np.moveaxis(np.asarray(x, np.float32).astype(ml_dtypes.bfloat16).astype(np.float64), axis, -1)
    blocks = v.reshape(v.shape[:-1] + (-1, 32))
    amax = np.abs(blocks).max(-1, keepdims=True)
    byte = np.maximum(np.where(amax > 0, np.frexp(amax)[1] - 1 + 127, 0) - down, 1)
    scale = np.exp2(byte - 127.0)
    codes = (blocks / scale).astype(np.float32).astype(dtype).astype(np.float64)
    return np.moveaxis((codes * scale).reshape(v.shape), -1, axis)


WIDE = False


def mx_kscale(k):
    if not WIDE:
        return np.ones(k)
    levels = np.array([10, -10, 5, -5, 0])
    if k % 512:
        return np.exp2(np.random.permutation(np.resize(levels, k // 32))).repeat(32)
    a = np.empty((k // 512, 16))
    for p in range(k // 512):
        a[p, :8] = np.random.permutation(np.resize(levels, 8))
        for g in range(8):
            far = levels[np.abs(levels - a[p, g]) >= 10]
            a[p, g + 8] = far[np.random.randint(len(far))]
    return np.exp2(a.ravel()).repeat(32)


def f64(x):
    return np.asarray(x).astype(np.float64)


def striped(idx):
    return np.tile(idx.reshape(-1, 16).T, (8, 1)).astype(np.uint16)


def unstriped(offs):
    return offs[:16].T.reshape(-1).astype(np.int64)


E2M1 = np.array([0.0, 0.5, 1.0, 1.5, 2.0, 3.0, 4.0, 6.0, -0.0, -0.5, -1.0, -1.5, -2.0, -3.0, -4.0, -6.0])


def pack_weight(w, fmt):
    k, n = w.shape
    w = f64(np.asarray(w, np.float32).astype(ml_dtypes.bfloat16)).reshape(k // 32, 32, n)
    amax = np.abs(w).max(1)
    if fmt == "e4m3":
        byte = np.frexp(amax)[1] - 1 + 127 - 7
    else:
        mant, ex = np.frexp(amax / 6.0)
        byte = np.where(mant > 0.5, ex, ex - 1) + 127
    byte = np.clip(np.where(amax > 0, byte, 1), 1, 254)
    scaled = (w * np.exp2(127.0 - byte)[:, None, :]).reshape(k, n).astype(np.float32)
    by_word = np.ascontiguousarray(scaled.reshape(k // 512, 128, 4, n).transpose(0, 1, 3, 2))
    if fmt == "e4m3":
        words = by_word.astype(ml_dtypes.float8_e4m3fn).view(np.uint8)
    else:
        c = by_word.astype(ml_dtypes.float4_e2m1fn).view(np.uint8) & 0xF
        words = (c[..., 0::2] | (c[..., 1::2] << 4)).reshape(k // 512, 128, 2 * n)
    return np.ascontiguousarray(words), np.ascontiguousarray(byte.astype(np.uint8).reshape(k // 512, 16, n))


def unpack_weight(words, scales, fmt):
    g, _, n = scales.shape
    words = np.ascontiguousarray(words).reshape(g, 128, n, -1)
    if fmt == "e4m3":
        vals = words.view(ml_dtypes.float8_e4m3fn).astype(np.float64)
    else:
        nib = np.empty((g, 128, n, 4), np.uint8)
        nib[..., 0::2] = words & 0xF
        nib[..., 1::2] = words >> 4
        vals = E2M1[nib]
    vals = vals * np.repeat(np.exp2(scales.astype(np.float64) - 127.0), 8, axis=1)[..., None]
    return vals.transpose(0, 1, 3, 2).reshape(g * 512, n)


def gelu(v):
    return 0.5 * v * (1.0 + np.tanh(np.sqrt(2.0 / np.pi) * (v + 0.044715 * v**3)))


def striped8(idx):
    return np.concatenate([v.reshape(-1, 16).T for v in idx]).astype(np.uint16)


def unstriped8(offs):
    return np.stack([offs[16 * g:16 * g + 16].T.reshape(-1) for g in range(8)]).astype(np.int64)


def put_heads(h, wgs, idx8, t2):
    r = np.arange(h.shape[0])
    page = np.zeros((h.shape[0], t2))
    page[r[:, None], idx8[r % 512 // 64]] = wgs[r // 4 % 128] * h
    return page


K, H, N, T, S, T2, P = 512, 1024, 512, 4096, 1024, 2048, 1024

def setup_inputs():
    n = np.random.standard_normal
    s = mx_kscale(K)[:, None]
    u = mx_kscale(H)[:, None]
    tab_words, tab_scales = pack_weight(n((K, T)) * s, "e4m3")
    w1_words, w1_scales = pack_weight(n((K, H)) / s / np.sqrt(K), "e2m1")
    w4_words, w4_scales = pack_weight(n((H, N)) / u / np.sqrt(H), "e4m3")
    return {
        "tab_words": tab_words, "tab_scales": tab_scales,
        "offs": striped(np.random.permutation(T)[:S]),
        "w1_words": w1_words, "w1_scales": w1_scales,
        "w2": (2.0 * n((K, H)) / s / np.sqrt(K)).astype(np.float32),
        "lev": (0.8 * n((H, S))).astype(np.float32),
        "wgs": np.repeat(np.random.uniform(0.5, 2.0, (8, S)), 16, axis=0).astype(np.float32),
        "offs2": striped8(np.stack([np.random.permutation(T2)[:S] for _ in range(8)])),
        "offs3": striped(np.random.permutation(T2)[:P]),
        "mask": n((H, P)).astype(np.float32),
        "gain": (np.exp(0.3 * n(H)) * u[:, 0]).astype(np.float32),
        "w3": (n((H, N)) / u / np.sqrt(H)).astype(np.float32),
        "w4_words": w4_words, "w4_scales": w4_scales,
    }

def reference(tab_words, tab_scales, offs, w1_words, w1_scales, w2, lev, wgs, offs2, offs3, mask, gain, w3, w4_words, w4_scales):
    v = unpack_weight(tab_words, tab_scales, "e4m3")[:, unstriped(offs)]
    w1 = unpack_weight(w1_words, w1_scales, "e2m1")
    w4 = unpack_weight(w4_words, w4_scales, "e4m3")
    h = (w1.T @ v) * f64(lev) + np.tanh(mxq(f64(w2), 0, "e4m3").T @ v)
    page = put_heads(h, f64(wgs), unstriped8(offs2), T2)
    x = page[:, unstriped(offs3)] + f64(mask)
    z = f64(gain)[:, None] * (x / (1.0 + np.exp(-x)))
    zq = mxq(z, 0, "e4m3")
    y1 = mxq(f64(w3), 0, "e4m3").T @ zq
    y2 = w4.T @ zq
    return np.maximum(y1, y2)

@@ -1,0 +1,289 @@
+from contextlib import ExitStack
+
+import concourse.mybir as mybir
+
+K, H, N, T, S, T2, M = 512, 1024, 512, 4096, 1024, 2048, 1024
+FLOPS = 2 * (2 * K * H * S + 2 * H * N * M)
+
+F32 = mybir.dt.float32
+BF16 = mybir.dt.bfloat16
+I32 = mybir.dt.int32
+U32 = mybir.dt.uint32
+U16 = mybir.dt.uint16
+U8 = mybir.dt.uint8
+FP8X4 = mybir.dt.float8_e4m3fn_x4
+FP4X4 = mybir.dt.float4_e2m1fn_x4
+ACT = mybir.ActivationFunctionType
+ALU = mybir.AluOpType
+
+P = 128
+PACK = 4
+BANK = 512
+PASSES = H // (P * PACK)
+SLICES = PASSES * PACK
+PER_COL = 16
+CHUNKS = (256, 256, 256, 128, 128)
+
+
+def tile_list_combiner_intermod_watch_kernel(
+    tc, tab_words, tab_scales, offs, w1_words, w1_scales, w2, lev, wgs, offs2, offs3, mask, gain, w3, w4_words,
+    w4_scales, out
+):
+    nc = tc.nc
+    with ExitStack() as ctx:
+        lists = ctx.enter_context(tc.tile_pool(name="lists", bufs=1))
+        keep = ctx.enter_context(tc.tile_pool(name="keep", bufs=1))
+        shared = ctx.enter_context(tc.tile_pool(name="shared", bufs=1))
+        ring = ctx.enter_context(tc.tile_pool(name="ring", bufs=2))
+        psum = ctx.enter_context(tc.psum_pool(name="psum", bufs=1))
+
+        def bank(n, shape):
+            return psum.tile(shape, F32, name="bank%d" % n, tag="bank%d" % n)
+
+        def load_scale_rows(queue, plane, rows):
+            for q in range(4):
+                queue.dma_start(out=plane[32 * q : 32 * q + 4].bitcast(I32), in_=rows[4 * q : 4 * q + 4].bitcast(I32))
+
+        tab_s = keep.tile([P, T], U8, name="tab_s")
+        nc.vector.memset(tab_s[:].bitcast(I32), 0)
+        w1s_raw = shared.tile([P, H], U8, name="w1s_raw", offset=22 * 1024)
+        nc.gpsimd.memset(w1s_raw[:].bitcast(I32), 0)
+        load_scale_rows(nc.scalar, tab_s, tab_scales[0])
+        load_scale_rows(nc.gpsimd, w1s_raw, w1_scales[0])
+
+        idx = lists.tile([P, S // PER_COL], U16, name="idx")
+        idx2 = lists.tile([P, S // PER_COL], U16, name="idx2")
+        idx3 = lists.tile([P, M // PER_COL], U16, name="idx3")
+        nc.sync.dma_start(idx[:], offs)
+        w1_raw = shared.tile([P, 2 * H], U8, name="w1_raw", offset=20 * 1024)
+        nc.sync.dma_start(out=w1_raw[:].bitcast(I32), in_=w1_words[0].bitcast(I32))
+        tab_w = shared.tile([P, T], I32, name="tab_w", offset=0)
+        nc.sync.dma_start(out=tab_w[:], in_=tab_words[0].rearrange("p t i -> p (t i)").bitcast(I32))
+
+        w2_rows = w2.rearrange("(p j) c -> p j c", j=PACK)
+        w3_rows = w3.rearrange("(b p j) n -> b p j n", b=PASSES, j=PACK)
+        lev_rows = lev.rearrange("(b p i) j -> b i p j", b=PASSES, i=PACK)
+        mask_rows = mask.rearrange("(b p i) m -> b p i m", b=PASSES, i=PACK)
+
+        def load_weight(rows):
+            raw = ring.tile([P, PACK, BANK], F32, name="w_raw", tag="w_raw")
+            nc.sync.dma_start(out=raw[:], in_=rows)
+            return raw
+
+        w2_raw0 = load_weight(w2_rows[:, :, 0:BANK])
+        lev_t = [keep.tile([P, S], F32, name="lev%d" % s) for s in range(SLICES)]
+        wgs_t = keep.tile([P, S], F32, name="wgs_t")
+        nc.sync.dma_start(out=lev_t[0][:, 0:BANK], in_=lev_rows[0, 0][:, 0:BANK])
+        nc.sync.dma_start(out=wgs_t[:, 0:BANK], in_=wgs[:, 0:BANK])
+        nc.sync.dma_start(idx2[:], offs2)
+        nc.sync.dma_start(out=lev_t[0][:, BANK:S], in_=lev_rows[0, 0][:, BANK:S])
+        nc.sync.dma_start(out=wgs_t[:, BANK:S], in_=wgs[:, BANK:S])
+
+        pages = [keep.tile([P, T2], F32, name="page0")]
+        nc.vector.memset(pages[0][:], 0.0)
+
+        w1_q = keep.tile([P, 2 * H], U8, name="w1_q", align_bytes=64)
+        w1_s = keep.tile([P, H], U8, name="w1_s", align_bytes=64)
+        nc.vector.tensor_copy(
+            out=w1_q[:].bitcast(U16).rearrange("p (b t q) -> p b q t", b=PASSES, t=PACK),
+            in_=w1_raw[:].bitcast(U16).rearrange("p (b q t) -> p b q t", b=PASSES, t=PACK),
+        )
+        for b in range(PASSES):
+            cols = slice(b * BANK, (b + 1) * BANK)
+            nc.gpsimd.tensor_copy(
+                out=w1_s[:, cols].rearrange("p (t q) -> p q t", t=PACK),
+                in_=w1s_raw[:, cols].rearrange("p (q t) -> p q t", t=PACK),
+            )
+
+        def quantise(name, grouped, width):
+            codes = keep.tile([P, width], U32, name=name + "_q", align_bytes=64)
+            scales = keep.tile([P, width], U8, name=name + "_s", align_bytes=64)
+            nc.vector.quantize_mx(out=codes[:].bitcast(FP8X4), scales=scales[:], in_=grouped[:])
+            return codes, scales
+
+        def quantise_w2(b, raw, grouped, steps):
+            codes = keep.tile([P, BANK], U32, name="w2_q%d" % b, align_bytes=64)
+            scales = keep.tile([P, BANK], U8, name="w2_s%d" % b, align_bytes=64)
+            for t0, t1 in steps:
+                nc.scalar.copy(
+                    out=grouped[:].rearrange("p (t q j) -> p q j t", t=PACK, j=PACK)[:, :, :, t0:t1],
+                    in_=raw[:].rearrange("p j (q t) -> p q j t", t=PACK)[:, :, :, t0:t1],
+                )
+                nc.vector.quantize_mx(
+                    out=codes[:, t0 * P : t1 * P].bitcast(FP8X4),
+                    scales=scales[:, t0 * P : t1 * P],
+                    in_=grouped[:, t0 * BANK : t1 * BANK],
+                )
+            return codes, scales
+
+        def interleave(copy, grouped, planes):
+            copy(
+                out=grouped.rearrange("p (c e i) -> p c i e", e=4, i=PACK),
+                in_=planes.rearrange("p i (c e) -> p c i e", e=4),
+            )
+
+        w2_bf0 = shared.tile([P, PACK * BANK], BF16, name="w2_bf0", offset=16 * 1024, align_bytes=64)
+
+        v_q, v_s = [], []
+        for half in range(S // BANK):
+            cols = slice(half * BANK // PER_COL, (half + 1) * BANK // PER_COL)
+            v_s.append(keep.tile([P, BANK], U8, name="v_s%d" % half, align_bytes=64))
+            nc.vector.tensor_copy(out=v_s[half][:], in_=tab_s[:].indirect(idx[:, cols]))
+            v_q.append(keep.tile([P, BANK], U32, name="v_q%d" % half, align_bytes=64))
+            nc.vector.tensor_copy(out=v_q[half][:], in_=tab_w[:].bitcast(U32).indirect(idx[:, cols]))
+
+        w2_mx = [quantise_w2(0, w2_raw0, w2_bf0, ((0, 1), (1, PACK)))]
+
+        for n, at in ((1, 16 * 1024), (2, 0), (3, 8 * 1024)):
+            pages.append(shared.tile([P, T2], F32, name="page%d" % n, offset=at))
+            nc.gpsimd.memset(pages[n][:], 0.0)
+
+        gain_t = keep.tile([P, PASSES, PACK], F32, name="gain_t")
+        mask0 = [keep.tile([P, M], F32, name="mask0_%d" % i) for i in range(PACK)]
+        nc.sync.dma_start(out=lev_t[1][:], in_=lev_rows[0, 1])
+        nc.sync.dma_start(idx3[:], offs3)
+        nc.sync.dma_start(out=gain_t[:], in_=gain.rearrange("(b p i) -> p b i", b=PASSES, i=PACK))
+        for i in range(PACK):
+            nc.sync.dma_start(out=mask0[i][:], in_=mask_rows[0][:, i, :])
+            nc.sync.dma_start(out=lev_t[i + 2][:], in_=lev_rows[(i + 2) // PACK, (i + 2) % PACK])
+            if i == 1:
+                w2_raw1 = load_weight(w2_rows[:, :, BANK:H])
+        for s in range(6, SLICES):
+            nc.sync.dma_start(out=lev_t[s][:], in_=lev_rows[s // PACK, s % PACK])
+        w2_bf1 = ring.tile([P, PACK * BANK], BF16, name="w_bf", tag="w_bf", align_bytes=64)
+        w2_mx.append(quantise_w2(1, w2_raw1, w2_bf1, ((0, PACK),)))
+
+        w3_mx = []
+        for b in range(PASSES):
+            raw = load_weight(w3_rows[b])
+            grouped = ring.tile([P, PACK * N], BF16, name="w_bf", tag="w_bf", align_bytes=64)
+            interleave(nc.scalar.copy, grouped[:], raw[:])
+            w3_mx.append(quantise("w3_%d" % b, grouped, N))
+        w4_q = keep.tile([P, PASSES, N], I32, name="w4_q", align_bytes=64)
+        w4_s = keep.tile([P, PASSES, N], U8, name="w4_s", align_bytes=64)
+        nc.gpsimd.memset(w4_s[:].rearrange("p a n -> p (a n)").bitcast(I32), 0)
+        nc.sync.dma_start(out=w4_q[:], in_=w4_words.rearrange("a p c i -> p a (c i)").bitcast(I32))
+        load_scale_rows(nc.sync, w4_s, w4_scales.rearrange("a r c -> r a c"))
+        w4_mx = [(w4_q[:, b, :], w4_s[:, b, :]) for b in range(PASSES)]
+        starts = [sum(CHUNKS[:c]) for c in range(len(CHUNKS))]
+        mask1 = []
+        for c, width in enumerate(CHUNKS):
+            mask1.append(keep.tile([P, PACK, width], F32, name="mask1_%d" % c))
+            nc.sync.dma_start(out=mask1[c][:], in_=mask_rows[1][:, :, starts[c] : starts[c] + width])
+
+        def features(s):
+            b, t = divmod(s, PACK)
+            h = ring.tile([P, S], F32, name="h", tag="h")
+            th = ring.tile([P, S], F32, name="th", tag="th")
+            for half in range(S // BANK):
+                cols = slice(half * BANK, (half + 1) * BANK)
+                p2 = bank(4 * (s % 2) + 2 * half, [P, BANK])
+                p1 = bank(4 * (s % 2) + 2 * half + 1, [P, BANK])
+                nc.tensor.matmul_mx(
+                    out=p2[:],
+                    lhsT=w2_mx[b][0][:, t * P : (t + 1) * P].bitcast(FP8X4),
+                    lhsT_scale=w2_mx[b][1][:, t * P : (t + 1) * P],
+                    rhs=v_q[half][:].bitcast(FP8X4),
+                    rhs_scale=v_s[half][:],
+                    start=True,
+                    stop=True,
+                )
+                nc.tensor.matmul_mx(
+                    out=p1[:],
+                    lhsT=w1_q[:, 2 * s * P : 2 * (s + 1) * P].bitcast(FP4X4),
+                    lhsT_scale=w1_s[:, s * P : (s + 1) * P],
+                    rhs=v_q[half][:].bitcast(FP8X4),
+                    rhs_scale=v_s[half][:],
+                    start=True,
+                    stop=True,
+                )
+                nc.scalar.activation(out=th[:, cols], in_=p2[:], func=ACT.Tanh)
+                nc.vector.tensor_tensor(out=h[:, cols], in0=p1[:], in1=lev_t[s][:, cols], op=ALU.mult)
+            return h, th
+
+        def place(s, h, th):
+            pieces = 2 if s == 0 else 1
+            width = S // pieces
+            for piece in range(pieces):
+                cols = slice(piece * width, (piece + 1) * width)
+                nc.vector.tensor_tensor(out=h[:, cols], in0=h[:, cols], in1=th[:, cols], op=ALU.add)
+            for piece in range(pieces):
+                cols = slice(piece * width, (piece + 1) * width)
+                entries = idx2[:, piece * width // PER_COL : (piece + 1) * width // PER_COL]
+                nc.vector.tensor_tensor(
+                    out=pages[s % PACK][:].indirect(entries), in0=h[:, cols], in1=wgs_t[:, cols], op=ALU.mult
+                )
+
+        def gain_and_round(planes, x, b, i):
+            nc.scalar.activation(out=planes, in_=x, func=ACT.Copy, scale=gain_t[:, b, i : i + 1])
+
+        z0_planes = keep.tile([P, PACK, M], BF16, name="z0_planes")
+
+        def pick0(i):
+            x = ring.tile([P, M], F32, name="x", tag="x")
+            nc.vector.tensor_tensor(out=x[:], in0=pages[i][:].indirect(idx3[:]), in1=mask0[i][:], op=ALU.add)
+            nc.scalar.activation(out=x[:], in_=x[:], func=ACT.Silu)
+            gain_and_round(z0_planes[:, i, :], x[:], 0, i)
+
+        z0 = []
+        pending = features(0)
+        for s in range(SLICES):
+            now = pending
+            if s + 1 < SLICES:
+                pending = features(s + 1)
+            place(s, *now)
+            if s < PACK:
+                pick0(s)
+            if s == PACK - 1:
+                for half in range(M // BANK):
+                    grouped = ring.tile([P, PACK * BANK], BF16, name="w_bf", tag="w_bf", align_bytes=64)
+                    interleave(nc.scalar.copy, grouped[:], z0_planes[:, :, half * BANK : (half + 1) * BANK])
+                    z0.append(quantise("z0_%d" % half, grouped, BANK))
+
+        out_rows = out.rearrange("(t p) m -> p t m", p=P)
+        n_tiles = N // P
+        next_bank = 0
+        for c, width in enumerate(CHUNKS):
+            x = ring.tile([P, PACK, BANK // 2], F32, name="h", tag="h")
+            entries = idx3[:, starts[c] // PER_COL : (starts[c] + width) // PER_COL]
+            xc = x[:].rearrange("p i m -> p (i m)")[:, 0 : PACK * width].rearrange("p (i m) -> p i m", i=PACK)
+            for i in range(PACK):
+                nc.vector.tensor_tensor(
+                    out=xc[:, i, :], in0=pages[i][:].indirect(entries), in1=mask1[c][:, i, :], op=ALU.add
+                )
+            nc.scalar.activation(out=xc, in_=xc, func=ACT.Silu)
+            planes = ring.tile([P, PACK, width], BF16, name="z1_planes", tag="z1_planes")
+            for i in range(PACK):
+                gain_and_round(planes[:, i, :], xc[:, i, :], 1, i)
+            grouped = ring.tile([P, PACK * width], BF16, name="z1_bf", tag="z1_bf", align_bytes=64)
+            interleave(nc.vector.tensor_copy, grouped[:], planes[:])
+            z1_q, z1_s = quantise("z1_%d" % c, grouped, width)
+            at = starts[c] % BANK
+            z0_q, z0_s = z0[starts[c] // BANK]
+            z_mx = [(z0_q[:, at : at + width], z0_s[:, at : at + width]), (z1_q[:], z1_s[:])]
+            per_bank = BANK // width
+            for first in range(0, n_tiles, per_bank):
+                sums = []
+                for weights in (w4_mx, w3_mx):
+                    acc = bank(next_bank % 8, [P, per_bank, width])
+                    next_bank = next_bank + 1
+                    for b in range(PASSES):
+                        for g in range(per_bank):
+                            n_cols = slice((first + g) * P, (first + g + 1) * P)
+                            nc.tensor.matmul_mx(
+                                out=acc[:, g, :],
+                                lhsT=weights[b][0][:, n_cols].bitcast(FP8X4),
+                                lhsT_scale=weights[b][1][:, n_cols],
+                                rhs=z_mx[b][0].bitcast(FP8X4),
+                                rhs_scale=z_mx[b][1],
+                                start=(b == 0 and g == 0),
+                                stop=(b == PASSES - 1 and g == per_bank - 1),
+                            )
+                    sums.append(acc)
+                y2 = ring.tile([P, per_bank, width], F32, name="y2", tag="y2")
+                nc.scalar.copy(out=y2[:], in_=sums[0][:])
+                y = ring.tile([P, per_bank, width], F32, name="y", tag="y", bufs=4)
+                nc.vector.tensor_tensor(out=y[:], in0=sums[1][:], in1=y2[:], op=ALU.max)
+                nc.sync.dma_start(
+                    out=out_rows[:, first : first + per_bank, starts[c] : starts[c] + width], in_=y[:]
+                )

@@ -22,7 +22,7 @@ BANK = 512
 PASSES = H // (P * PACK)
 SLICES = PASSES * PACK
 PER_COL = 16
-CHUNKS = (256, 256, 256, 128, 128)
+CHUNKS = (128, 128, 256, 256, 256)
 
 
 def tile_list_combiner_intermod_watch_kernel(
@@ -33,7 +33,6 @@ def tile_list_combiner_intermod_watch_kernel(
     with ExitStack() as ctx:
         lists = ctx.enter_context(tc.tile_pool(name="lists", bufs=1))
         keep = ctx.enter_context(tc.tile_pool(name="keep", bufs=1))
-        shared = ctx.enter_context(tc.tile_pool(name="shared", bufs=1))
         ring = ctx.enter_context(tc.tile_pool(name="ring", bufs=2))
         psum = ctx.enter_context(tc.psum_pool(name="psum", bufs=1))
 
@@ -46,7 +45,7 @@ def tile_list_combiner_intermod_watch_kernel(
 
         tab_s = keep.tile([P, T], U8, name="tab_s")
         nc.vector.memset(tab_s[:].bitcast(I32), 0)
-        w1s_raw = shared.tile([P, H], U8, name="w1s_raw", offset=22 * 1024)
+        w1s_raw = keep.tile([P, H], U8, name="w1s_raw")
         nc.gpsimd.memset(w1s_raw[:].bitcast(I32), 0)
         load_scale_rows(nc.scalar, tab_s, tab_scales[0])
         load_scale_rows(nc.gpsimd, w1s_raw, w1_scales[0])
@@ -55,15 +54,15 @@ def tile_list_combiner_intermod_watch_kernel(
         idx2 = lists.tile([P, S // PER_COL], U16, name="idx2")
         idx3 = lists.tile([P, M // PER_COL], U16, name="idx3")
         nc.sync.dma_start(idx[:], offs)
-        w1_raw = shared.tile([P, 2 * H], U8, name="w1_raw", offset=20 * 1024)
+        w1_raw = keep.tile([P, 2 * H], U8, name="w1_raw")
         nc.sync.dma_start(out=w1_raw[:].bitcast(I32), in_=w1_words[0].bitcast(I32))
-        tab_w = shared.tile([P, T], I32, name="tab_w", offset=0)
+        tab_w = keep.tile([P, T], I32, name="tab_w")
         nc.sync.dma_start(out=tab_w[:], in_=tab_words[0].rearrange("p t i -> p (t i)").bitcast(I32))
 
         w2_rows = w2.rearrange("(p j) c -> p j c", j=PACK)
         w3_rows = w3.rearrange("(b p j) n -> b p j n", b=PASSES, j=PACK)
         lev_rows = lev.rearrange("(b p i) j -> b i p j", b=PASSES, i=PACK)
-        mask_rows = mask.rearrange("(b p i) m -> b p i m", b=PASSES, i=PACK)
+        mask_rows = mask.rearrange("(b p i) m -> b i p m", b=PASSES, i=PACK)
 
         def load_weight(rows):
             raw = ring.tile([P, PACK, BANK], F32, name="w_raw", tag="w_raw")
@@ -79,8 +78,8 @@ def tile_list_combiner_intermod_watch_kernel(
         nc.sync.dma_start(out=lev_t[0][:, BANK:S], in_=lev_rows[0, 0][:, BANK:S])
         nc.sync.dma_start(out=wgs_t[:, BANK:S], in_=wgs[:, BANK:S])
 
-        pages = [keep.tile([P, T2], F32, name="page0")]
-        nc.vector.memset(pages[0][:], 0.0)
+        page = keep.tile([P, T2], F32, name="page")
+        nc.vector.memset(page[:], 0.0)
 
         w1_q = keep.tile([P, 2 * H], U8, name="w1_q", align_bytes=64)
         w1_s = keep.tile([P, H], U8, name="w1_s", align_bytes=64)
@@ -98,7 +97,7 @@ def tile_list_combiner_intermod_watch_kernel(
         def quantise(name, grouped, width):
             codes = keep.tile([P, width], U32, name=name + "_q", align_bytes=64)
             scales = keep.tile([P, width], U8, name=name + "_s", align_bytes=64)
-            nc.vector.quantize_mx(out=codes[:].bitcast(FP8X4), scales=scales[:], in_=grouped[:])
+            nc.vector.quantize_mx(out=codes[:].bitcast(FP8X4), scales=scales[:], in_=grouped)
             return codes, scales
 
         def quantise_w2(b, raw, grouped, steps):
@@ -122,7 +121,7 @@ def tile_list_combiner_intermod_watch_kernel(
                 in_=planes.rearrange("p i (c e) -> p c i e", e=4),
             )
 
-        w2_bf0 = shared.tile([P, PACK * BANK], BF16, name="w2_bf0", offset=16 * 1024, align_bytes=64)
+        w2_bf0 = keep.tile([P, PACK * BANK], BF16, name="w2_bf0", align_bytes=64)
 
         v_q, v_s = [], []
         for half in range(S // BANK):
@@ -134,47 +133,44 @@ def tile_list_combiner_intermod_watch_kernel(
 
         w2_mx = [quantise_w2(0, w2_raw0, w2_bf0, ((0, 1), (1, PACK)))]
 
-        for n, at in ((1, 16 * 1024), (2, 0), (3, 8 * 1024)):
-            pages.append(shared.tile([P, T2], F32, name="page%d" % n, offset=at))
-            nc.gpsimd.memset(pages[n][:], 0.0)
-
         gain_t = keep.tile([P, PASSES, PACK], F32, name="gain_t")
-        mask0 = [keep.tile([P, M], F32, name="mask0_%d" % i) for i in range(PACK)]
+        mask_t = [keep.tile([P, M], F32, name="mask%d" % s) for s in range(SLICES)]
         nc.sync.dma_start(out=lev_t[1][:], in_=lev_rows[0, 1])
         nc.sync.dma_start(idx3[:], offs3)
         nc.sync.dma_start(out=gain_t[:], in_=gain.rearrange("(b p i) -> p b i", b=PASSES, i=PACK))
-        for i in range(PACK):
-            nc.sync.dma_start(out=mask0[i][:], in_=mask_rows[0][:, i, :])
-            nc.sync.dma_start(out=lev_t[i + 2][:], in_=lev_rows[(i + 2) // PACK, (i + 2) % PACK])
-            if i == 1:
-                w2_raw1 = load_weight(w2_rows[:, :, BANK:H])
-        for s in range(6, SLICES):
-            nc.sync.dma_start(out=lev_t[s][:], in_=lev_rows[s // PACK, s % PACK])
+
+        def load_rows(slices):
+            for s in slices:
+                nc.sync.dma_start(out=mask_t[s][:], in_=mask_rows[s // PACK, s % PACK])
+                if s + 2 < SLICES:
+                    nc.sync.dma_start(out=lev_t[s + 2][:], in_=lev_rows[(s + 2) // PACK, (s + 2) % PACK])
+
+        load_rows(range(0, 2))
+        w2_raw1 = load_weight(w2_rows[:, :, BANK:H])
         w2_bf1 = ring.tile([P, PACK * BANK], BF16, name="w_bf", tag="w_bf", align_bytes=64)
         w2_mx.append(quantise_w2(1, w2_raw1, w2_bf1, ((0, PACK),)))
-
+        load_rows(range(2, 3))
         w3_mx = []
         for b in range(PASSES):
             raw = load_weight(w3_rows[b])
             grouped = ring.tile([P, PACK * N], BF16, name="w_bf", tag="w_bf", align_bytes=64)
             interleave(nc.scalar.copy, grouped[:], raw[:])
-            w3_mx.append(quantise("w3_%d" % b, grouped, N))
+            w3_mx.append(quantise("w3_%d" % b, grouped[:], N))
+        load_rows(range(3, 4))
         w4_q = keep.tile([P, PASSES, N], I32, name="w4_q", align_bytes=64)
         w4_s = keep.tile([P, PASSES, N], U8, name="w4_s", align_bytes=64)
         nc.gpsimd.memset(w4_s[:].rearrange("p a n -> p (a n)").bitcast(I32), 0)
         nc.sync.dma_start(out=w4_q[:], in_=w4_words.rearrange("a p c i -> p a (c i)").bitcast(I32))
         load_scale_rows(nc.sync, w4_s, w4_scales.rearrange("a r c -> r a c"))
+        load_rows(range(4, SLICES))
         w4_mx = [(w4_q[:, b, :], w4_s[:, b, :]) for b in range(PASSES)]
         starts = [sum(CHUNKS[:c]) for c in range(len(CHUNKS))]
-        mask1 = []
-        for c, width in enumerate(CHUNKS):
-            mask1.append(keep.tile([P, PACK, width], F32, name="mask1_%d" % c))
-            nc.sync.dma_start(out=mask1[c][:], in_=mask_rows[1][:, :, starts[c] : starts[c] + width])
 
         def features(s):
             b, t = divmod(s, PACK)
             h = ring.tile([P, S], F32, name="h", tag="h")
             th = ring.tile([P, S], F32, name="th", tag="th")
+            in_bank = []
             for half in range(S // BANK):
                 cols = slice(half * BANK, (half + 1) * BANK)
                 p2 = bank(4 * (s % 2) + 2 * half, [P, BANK])
@@ -198,92 +194,124 @@ def tile_list_combiner_intermod_watch_kernel(
                     stop=True,
                 )
                 nc.scalar.activation(out=th[:, cols], in_=p2[:], func=ACT.Tanh)
+                if s >= 2 and half == 1:
+                    nc.scalar.copy(out=h[:, cols], in_=p1[:])
+                else:
+                    in_bank.append((cols, p1))
+            return h, th, in_bank
+
+        def times_lev(s, h, th, in_bank):
+            for cols, p1 in in_bank:
                 nc.vector.tensor_tensor(out=h[:, cols], in0=p1[:], in1=lev_t[s][:, cols], op=ALU.mult)
-            return h, th
 
-        def place(s, h, th):
-            pieces = 2 if s == 0 else 1
-            width = S // pieces
-            for piece in range(pieces):
-                cols = slice(piece * width, (piece + 1) * width)
-                nc.vector.tensor_tensor(out=h[:, cols], in0=h[:, cols], in1=th[:, cols], op=ALU.add)
-            for piece in range(pieces):
-                cols = slice(piece * width, (piece + 1) * width)
-                entries = idx2[:, piece * width // PER_COL : (piece + 1) * width // PER_COL]
-                nc.vector.tensor_tensor(
-                    out=pages[s % PACK][:].indirect(entries), in0=h[:, cols], in1=wgs_t[:, cols], op=ALU.mult
-                )
+        def place(s, h, th, in_bank):
+            halves = [slice(half * BANK, (half + 1) * BANK) for half in range(S // BANK)]
+            if s == 0:
+                for half, cols in enumerate(halves):
+                    engine = nc.vector if half == 0 else nc.gpsimd
+                    engine.tensor_tensor(out=h[:, cols], in0=h[:, cols], in1=th[:, cols], op=ALU.add)
+                    engine.tensor_tensor(out=h[:, cols], in0=h[:, cols], in1=wgs_t[:, cols], op=ALU.mult)
+                    entries = idx2[:, half * BANK // PER_COL : (half + 1) * BANK // PER_COL]
+                    nc.vector.tensor_copy(out=page[:].indirect(entries), in_=h[:, cols])
+                return
+            if s == 1:
+                nc.gpsimd.tensor_tensor(out=h[:], in0=h[:], in1=th[:], op=ALU.add)
+            else:
+                first, second = halves
+                nc.gpsimd.tensor_tensor(out=h[:, first], in0=h[:, first], in1=th[:, first], op=ALU.add)
+                nc.gpsimd.tensor_tensor(out=h[:, second], in0=h[:, second], in1=lev_t[s][:, second], op=ALU.mult)
+                nc.gpsimd.tensor_tensor(out=h[:, second], in0=h[:, second], in1=th[:, second], op=ALU.add)
+            nc.gpsimd.tensor_tensor(out=h[:], in0=h[:], in1=wgs_t[:], op=ALU.mult)
+            nc.vector.tensor_copy(out=page[:].indirect(idx2[:]), in_=h[:])
 
-        def gain_and_round(planes, x, b, i):
-            nc.scalar.activation(out=planes, in_=x, func=ACT.Copy, scale=gain_t[:, b, i : i + 1])
+        z_parts = [
+            [(at, BANK) for at in range(0, M, BANK)],
+            [(starts[c], width) for c, width in enumerate(CHUNKS)],
+        ]
+        z_bf = [
+            [keep.tile([P, width, PACK], BF16, name="z_bf%d_%d" % (b, at), align_bytes=64) for at, width in z_parts[b]]
+            for b in range(PASSES)
+        ]
 
-        z0_planes = keep.tile([P, PACK, M], BF16, name="z0_planes")
-
-        def pick0(i):
-            x = ring.tile([P, M], F32, name="x", tag="x")
-            nc.vector.tensor_tensor(out=x[:], in0=pages[i][:].indirect(idx3[:]), in1=mask0[i][:], op=ALU.add)
+        def pick(s, at, width, tag, bufs):
+            x = ring.tile([P, width], F32, name=tag, tag=tag, bufs=bufs)
+            entries = idx3[:, at // PER_COL : (at + width) // PER_COL]
+            nc.vector.tensor_tensor(
+                out=x[:], in0=page[:].indirect(entries), in1=mask_t[s][:, at : at + width], op=ALU.add
+            )
             nc.scalar.activation(out=x[:], in_=x[:], func=ACT.Silu)
-            gain_and_round(z0_planes[:, i, :], x[:], 0, i)
+            return x
+
+        def gain_and_round(s, part, x):
+            b, i = divmod(s, PACK)
+            nc.scalar.activation(out=z_bf[b][part][:, :, i], in_=x, func=ACT.Copy, scale=gain_t[:, b, i : i + 1])
+
+        units = [
+            (c, first, BANK // width) for c, width in enumerate(CHUNKS) for first in range(0, N // P, BANK // width)
+        ]
+
+        def score_pass(n, sums, b, z_q, z_s):
+            c, first, per_bank = units[n]
+            for acc, weights in zip(sums, (w4_mx, w3_mx)):
+                for g in range(per_bank):
+                    n_cols = slice((first + g) * P, (first + g + 1) * P)
+                    nc.tensor.matmul_mx(
+                        out=acc[:, g, :],
+                        lhsT=weights[b][0][:, n_cols].bitcast(FP8X4),
+                        lhsT_scale=weights[b][1][:, n_cols],
+                        rhs=z_q.bitcast(FP8X4),
+                        rhs_scale=z_s,
+                        start=(b == 0 and g == 0),
+                        stop=(b == PASSES - 1 and g == per_bank - 1),
+                    )
+
+        def first_pass(n):
+            c, first, per_bank = units[n]
+            sums = [bank((2 * n + k) % 8, [P, per_bank, CHUNKS[c]]) for k in range(2)]
+            z_q, z_s = z0[starts[c] // BANK]
+            cols = slice(starts[c] % BANK, starts[c] % BANK + CHUNKS[c])
+            score_pass(n, sums, 0, z_q[:, cols], z_s[:, cols])
+            return sums
 
         z0 = []
-        pending = features(0)
+        made = [features(0), features(1)]
+        times_lev(0, *made[0])
+        times_lev(1, *made[1])
         for s in range(SLICES):
-            now = pending
+            if s == SLICES - 1:
+                opened = [first_pass(n) for n in range(4)]
+            place(s, *made[s])
+            if s + 2 < SLICES:
+                made.append(features(s + 2))
             if s + 1 < SLICES:
-                pending = features(s + 1)
-            place(s, *now)
-            if s < PACK:
-                pick0(s)
+                x = pick(s, 0, M, "x", 2)
+                for part, (at, width) in enumerate(z_parts[s // PACK]):
+                    gain_and_round(s, part, x[:, at : at + width])
+            if s + 2 < SLICES:
+                times_lev(s + 2, *made[s + 2])
             if s == PACK - 1:
-                for half in range(M // BANK):
-                    grouped = ring.tile([P, PACK * BANK], BF16, name="w_bf", tag="w_bf", align_bytes=64)
-                    interleave(nc.scalar.copy, grouped[:], z0_planes[:, :, half * BANK : (half + 1) * BANK])
-                    z0.append(quantise("z0_%d" % half, grouped, BANK))
+                for part in range(M // BANK):
+                    z0.append(quantise("z0_%d" % part, z_bf[0][part][:].rearrange("p m i -> p (m i)"), BANK))
+
+        def last_pick(c):
+            x = pick(SLICES - 1, starts[c], CHUNKS[c], "x_last", len(CHUNKS))
+            gain_and_round(SLICES - 1, c, x[:])
+            return quantise("z1_%d" % c, z_bf[1][c][:].rearrange("p m i -> p (m i)"), CHUNKS[c])
+
+        z1 = [last_pick(0)]
 
         out_rows = out.rearrange("(t p) m -> p t m", p=P)
-        n_tiles = N // P
-        next_bank = 0
-        for c, width in enumerate(CHUNKS):
-            x = ring.tile([P, PACK, BANK // 2], F32, name="h", tag="h")
-            entries = idx3[:, starts[c] // PER_COL : (starts[c] + width) // PER_COL]
-            xc = x[:].rearrange("p i m -> p (i m)")[:, 0 : PACK * width].rearrange("p (i m) -> p i m", i=PACK)
-            for i in range(PACK):
-                nc.vector.tensor_tensor(
-                    out=xc[:, i, :], in0=pages[i][:].indirect(entries), in1=mask1[c][:, i, :], op=ALU.add
-                )
-            nc.scalar.activation(out=xc, in_=xc, func=ACT.Silu)
-            planes = ring.tile([P, PACK, width], BF16, name="z1_planes", tag="z1_planes")
-            for i in range(PACK):
-                gain_and_round(planes[:, i, :], xc[:, i, :], 1, i)
-            grouped = ring.tile([P, PACK * width], BF16, name="z1_bf", tag="z1_bf", align_bytes=64)
-            interleave(nc.vector.tensor_copy, grouped[:], planes[:])
-            z1_q, z1_s = quantise("z1_%d" % c, grouped, width)
-            at = starts[c] % BANK
-            z0_q, z0_s = z0[starts[c] // BANK]
-            z_mx = [(z0_q[:, at : at + width], z0_s[:, at : at + width]), (z1_q[:], z1_s[:])]
-            per_bank = BANK // width
-            for first in range(0, n_tiles, per_bank):
-                sums = []
-                for weights in (w4_mx, w3_mx):
-                    acc = bank(next_bank % 8, [P, per_bank, width])
-                    next_bank = next_bank + 1
-                    for b in range(PASSES):
-                        for g in range(per_bank):
-                            n_cols = slice((first + g) * P, (first + g + 1) * P)
-                            nc.tensor.matmul_mx(
-                                out=acc[:, g, :],
-                                lhsT=weights[b][0][:, n_cols].bitcast(FP8X4),
-                                lhsT_scale=weights[b][1][:, n_cols],
-                                rhs=z_mx[b][0].bitcast(FP8X4),
-                                rhs_scale=z_mx[b][1],
-                                start=(b == 0 and g == 0),
-                                stop=(b == PASSES - 1 and g == per_bank - 1),
-                            )
-                    sums.append(acc)
-                y2 = ring.tile([P, per_bank, width], F32, name="y2", tag="y2")
-                nc.scalar.copy(out=y2[:], in_=sums[0][:])
-                y = ring.tile([P, per_bank, width], F32, name="y", tag="y", bufs=4)
-                nc.vector.tensor_tensor(out=y[:], in0=sums[1][:], in1=y2[:], op=ALU.max)
-                nc.sync.dma_start(
-                    out=out_rows[:, first : first + per_bank, starts[c] : starts[c] + width], in_=y[:]
-                )
+        for n, (c, first, per_bank) in enumerate(units):
+            if first == 0 and c + 1 < len(CHUNKS):
+                z1.append(last_pick(c + 1))
+            if n >= len(opened):
+                opened.append(first_pass(n))
+            sums = opened[n]
+            score_pass(n, sums, 1, z1[c][0][:], z1[c][1][:])
+            y2 = ring.tile([P, per_bank, CHUNKS[c]], F32, name="y2", tag="y2")
+            nc.scalar.copy(out=y2[:], in_=sums[0][:])
+            y = ring.tile([P, per_bank, CHUNKS[c]], F32, name="y", tag="y", bufs=4)
+            nc.vector.tensor_tensor(out=y[:], in0=sums[1][:], in1=y2[:], op=ALU.max)
+            nc.sync.dma_start(
+                out=out_rows[:, first : first + per_bank, starts[c] : starts[c] + CHUNKS[c]], in_=y[:]
+            )

@@ -1,6 +1,7 @@
 from contextlib import ExitStack
 
 import concourse.mybir as mybir
+from concourse.masks import make_identity
 
 K, H, N, T, S, T2, M = 512, 1024, 512, 4096, 1024, 2048, 1024
 FLOPS = 2 * (2 * K * H * S + 2 * H * N * M)
@@ -22,6 +23,11 @@ BANK = 512
 PASSES = H // (P * PACK)
 SLICES = PASSES * PACK
 PER_COL = 16
+VECTOR_HALVES = 3
+FUSED_FROM = 5
+PAGES = 2
+LATE_PICKS = range(2, 6)
+AHEAD = 5
 CHUNKS = (128, 128, 256, 256, 256)
 
 
@@ -33,6 +39,7 @@ def tile_list_combiner_intermod_watch_kernel(
     with ExitStack() as ctx:
         lists = ctx.enter_context(tc.tile_pool(name="lists", bufs=1))
         keep = ctx.enter_context(tc.tile_pool(name="keep", bufs=1))
+        reused = ctx.enter_context(tc.tile_pool(name="reused", bufs=1))
         ring = ctx.enter_context(tc.tile_pool(name="ring", bufs=2))
         psum = ctx.enter_context(tc.psum_pool(name="psum", bufs=1))
 
@@ -47,17 +54,16 @@ def tile_list_combiner_intermod_watch_kernel(
         nc.vector.memset(tab_s[:].bitcast(I32), 0)
         w1s_raw = keep.tile([P, H], U8, name="w1s_raw")
         nc.gpsimd.memset(w1s_raw[:].bitcast(I32), 0)
-        load_scale_rows(nc.scalar, tab_s, tab_scales[0])
-        load_scale_rows(nc.gpsimd, w1s_raw, w1_scales[0])
 
         idx = lists.tile([P, S // PER_COL], U16, name="idx")
         idx2 = lists.tile([P, S // PER_COL], U16, name="idx2")
         idx3 = lists.tile([P, M // PER_COL], U16, name="idx3")
         nc.sync.dma_start(idx[:], offs)
+        tab_s_rows = ring.tile([P, T], U8, name="tab_s_rows", tag="turned")
+        load_scale_rows(nc.sync, tab_s_rows, tab_scales[0])
+        load_scale_rows(nc.scalar, w1s_raw, w1_scales[0])
         w1_raw = keep.tile([P, 2 * H], U8, name="w1_raw")
         nc.sync.dma_start(out=w1_raw[:].bitcast(I32), in_=w1_words[0].bitcast(I32))
-        tab_w = keep.tile([P, T], I32, name="tab_w")
-        nc.sync.dma_start(out=tab_w[:], in_=tab_words[0].rearrange("p t i -> p (t i)").bitcast(I32))
 
         w2_rows = w2.rearrange("(p j) c -> p j c", j=PACK)
         w3_rows = w3.rearrange("(b p j) n -> b p j n", b=PASSES, j=PACK)
@@ -70,17 +76,23 @@ def tile_list_combiner_intermod_watch_kernel(
             return raw
 
         w2_raw0 = load_weight(w2_rows[:, :, 0:BANK])
-        lev_t = [keep.tile([P, S], F32, name="lev%d" % s) for s in range(SLICES)]
+        tab_w = reused.tile([P, T], I32, name="tab_w", offset=0, align_bytes=64)
+        nc.sync.dma_start(out=tab_w[:], in_=tab_words[0].rearrange("p t i -> p (t i)").bitcast(I32))
+        h_t = [keep.tile([P, S], F32, name="h%d" % s, tag="h%d" % s, align_bytes=64) for s in range(SLICES)]
         wgs_t = keep.tile([P, S], F32, name="wgs_t")
-        nc.sync.dma_start(out=lev_t[0][:, 0:BANK], in_=lev_rows[0, 0][:, 0:BANK])
+        nc.sync.dma_start(out=h_t[0][:, 0:BANK], in_=lev_rows[0, 0][:, 0:BANK])
         nc.sync.dma_start(out=wgs_t[:, 0:BANK], in_=wgs[:, 0:BANK])
         nc.sync.dma_start(idx2[:], offs2)
-        nc.sync.dma_start(out=lev_t[0][:, BANK:S], in_=lev_rows[0, 0][:, BANK:S])
+        nc.sync.dma_start(out=h_t[0][:, BANK:S], in_=lev_rows[0, 0][:, BANK:S])
         nc.sync.dma_start(out=wgs_t[:, BANK:S], in_=wgs[:, BANK:S])
 
-        page = keep.tile([P, T2], F32, name="page")
-        nc.vector.memset(page[:], 0.0)
+        pages = [keep.tile([P, T2], F32, name="page%d" % n) for n in range(PAGES)]
+        for page in pages:
+            nc.vector.memset(page[:], 0.0)
 
+        for q in range(4):
+            rows = slice(32 * q, 32 * q + 4)
+            nc.vector.tensor_copy(out=tab_s[rows].bitcast(I32), in_=tab_s_rows[rows].bitcast(I32))
         w1_q = keep.tile([P, 2 * H], U8, name="w1_q", align_bytes=64)
         w1_s = keep.tile([P, H], U8, name="w1_s", align_bytes=64)
         nc.vector.tensor_copy(
@@ -94,26 +106,19 @@ def tile_list_combiner_intermod_watch_kernel(
                 in_=w1s_raw[:, cols].rearrange("p (q t) -> p q t", t=PACK),
             )
 
-        def quantise(name, grouped, width):
-            codes = keep.tile([P, width], U32, name=name + "_q", align_bytes=64)
+        def quantise(name, grouped, width, tag):
+            codes = keep.tile([P, width], U32, name=name + "_q", tag=tag, align_bytes=64)
             scales = keep.tile([P, width], U8, name=name + "_s", align_bytes=64)
             nc.vector.quantize_mx(out=codes[:].bitcast(FP8X4), scales=scales[:], in_=grouped)
             return codes, scales
 
-        def quantise_w2(b, raw, grouped, steps):
-            codes = keep.tile([P, BANK], U32, name="w2_q%d" % b, align_bytes=64)
-            scales = keep.tile([P, BANK], U8, name="w2_s%d" % b, align_bytes=64)
-            for t0, t1 in steps:
-                nc.scalar.copy(
-                    out=grouped[:].rearrange("p (t q j) -> p q j t", t=PACK, j=PACK)[:, :, :, t0:t1],
-                    in_=raw[:].rearrange("p j (q t) -> p q j t", t=PACK)[:, :, :, t0:t1],
-                )
-                nc.vector.quantize_mx(
-                    out=codes[:, t0 * P : t1 * P].bitcast(FP8X4),
-                    scales=scales[:, t0 * P : t1 * P],
-                    in_=grouped[:, t0 * BANK : t1 * BANK],
-                )
-            return codes, scales
+        def round_w2(raw, tag):
+            grouped = keep.tile([P, PACK * BANK], BF16, name="w2_bf", tag=tag, align_bytes=64)
+            nc.scalar.copy(
+                out=grouped[:].rearrange("p (t q j) -> p q j t", t=PACK, j=PACK),
+                in_=raw[:].rearrange("p j (q t) -> p q j t", t=PACK),
+            )
+            return grouped
 
         def interleave(copy, grouped, planes):
             copy(
@@ -121,7 +126,7 @@ def tile_list_combiner_intermod_watch_kernel(
                 in_=planes.rearrange("p i (c e) -> p c i e", e=4),
             )
 
-        w2_bf0 = keep.tile([P, PACK * BANK], BF16, name="w2_bf0", align_bytes=64)
+        w2_mx = [quantise("w2_0", round_w2(w2_raw0, "w2_bf0")[:], BANK, "w2_0")]
 
         v_q, v_s = [], []
         for half in range(S // BANK):
@@ -131,11 +136,10 @@ def tile_list_combiner_intermod_watch_kernel(
             v_q.append(keep.tile([P, BANK], U32, name="v_q%d" % half, align_bytes=64))
             nc.vector.tensor_copy(out=v_q[half][:], in_=tab_w[:].bitcast(U32).indirect(idx[:, cols]))
 
-        w2_mx = [quantise_w2(0, w2_raw0, w2_bf0, ((0, 1), (1, PACK)))]
-
         gain_t = keep.tile([P, PASSES, PACK], F32, name="gain_t")
         mask_t = [keep.tile([P, M], F32, name="mask%d" % s) for s in range(SLICES)]
-        nc.sync.dma_start(out=lev_t[1][:], in_=lev_rows[0, 1])
+        nc.sync.dma_start(out=h_t[1][:], in_=lev_rows[0, 1])
+        w2_raw1 = load_weight(w2_rows[:, :, BANK:H])
         nc.sync.dma_start(idx3[:], offs3)
         nc.sync.dma_start(out=gain_t[:], in_=gain.rearrange("(b p i) -> p b i", b=PASSES, i=PACK))
 
@@ -143,38 +147,32 @@ def tile_list_combiner_intermod_watch_kernel(
             for s in slices:
                 nc.sync.dma_start(out=mask_t[s][:], in_=mask_rows[s // PACK, s % PACK])
                 if s + 2 < SLICES:
-                    nc.sync.dma_start(out=lev_t[s + 2][:], in_=lev_rows[(s + 2) // PACK, (s + 2) % PACK])
+                    nc.sync.dma_start(out=h_t[s + 2][:], in_=lev_rows[(s + 2) // PACK, (s + 2) % PACK])
 
-        load_rows(range(0, 2))
-        w2_raw1 = load_weight(w2_rows[:, :, BANK:H])
-        w2_bf1 = ring.tile([P, PACK * BANK], BF16, name="w_bf", tag="w_bf", align_bytes=64)
-        w2_mx.append(quantise_w2(1, w2_raw1, w2_bf1, ((0, PACK),)))
-        load_rows(range(2, 3))
-        w3_mx = []
+        load_rows(range(0, 3))
+        w3_bf = reused.tile([P, PASSES * PACK * N], BF16, name="w3_bf", offset=2 * T, align_bytes=64)
         for b in range(PASSES):
-            raw = load_weight(w3_rows[b])
-            grouped = ring.tile([P, PACK * N], BF16, name="w_bf", tag="w_bf", align_bytes=64)
-            interleave(nc.scalar.copy, grouped[:], raw[:])
-            w3_mx.append(quantise("w3_%d" % b, grouped[:], N))
-        load_rows(range(3, 4))
+            interleave(nc.scalar.copy, w3_bf[:, b * PACK * N : (b + 1) * PACK * N], load_weight(w3_rows[b])[:])
         w4_q = keep.tile([P, PASSES, N], I32, name="w4_q", align_bytes=64)
         w4_s = keep.tile([P, PASSES, N], U8, name="w4_s", align_bytes=64)
         nc.gpsimd.memset(w4_s[:].rearrange("p a n -> p (a n)").bitcast(I32), 0)
         nc.sync.dma_start(out=w4_q[:], in_=w4_words.rearrange("a p c i -> p a (c i)").bitcast(I32))
         load_scale_rows(nc.sync, w4_s, w4_scales.rearrange("a r c -> r a c"))
-        load_rows(range(4, SLICES))
+        load_rows(range(3, SLICES))
         w4_mx = [(w4_q[:, b, :], w4_s[:, b, :]) for b in range(PASSES)]
         starts = [sum(CHUNKS[:c]) for c in range(len(CHUNKS))]
 
+        ident = keep.tile([P, P], F32, name="ident")
+        make_identity(nc, ident[:])
+        halves = [slice(half * BANK, (half + 1) * BANK) for half in range(S // BANK)]
+
         def features(s):
             b, t = divmod(s, PACK)
-            h = ring.tile([P, S], F32, name="h", tag="h")
-            th = ring.tile([P, S], F32, name="th", tag="th")
-            in_bank = []
-            for half in range(S // BANK):
-                cols = slice(half * BANK, (half + 1) * BANK)
-                p2 = bank(4 * (s % 2) + 2 * half, [P, BANK])
-                p1 = bank(4 * (s % 2) + 2 * half + 1, [P, BANK])
+            th = ring.tile([P, S], F32, name="th", tag="th", bufs=AHEAD)
+            y1 = ring.tile([P, S], F32, name="y1", tag="y1", bufs=AHEAD)
+            for half, cols in enumerate(halves):
+                p2 = bank(2 * half, [P, BANK])
+                p1 = bank(2 * half + 1, [P, BANK])
                 nc.tensor.matmul_mx(
                     out=p2[:],
                     lhsT=w2_mx[b][0][:, t * P : (t + 1) * P].bitcast(FP8X4),
@@ -194,57 +192,78 @@ def tile_list_combiner_intermod_watch_kernel(
                     stop=True,
                 )
                 nc.scalar.activation(out=th[:, cols], in_=p2[:], func=ACT.Tanh)
-                if s >= 2 and half == 1:
-                    nc.scalar.copy(out=h[:, cols], in_=p1[:])
+                if 2 * s + half < VECTOR_HALVES:
+                    nc.vector.tensor_tensor(out=h_t[s][:, cols], in0=p1[:], in1=h_t[s][:, cols], op=ALU.mult)
                 else:
-                    in_bank.append((cols, p1))
-            return h, th, in_bank
+                    nc.scalar.copy(out=y1[:, cols], in_=p1[:])
+            return th, y1
 
-        def times_lev(s, h, th, in_bank):
-            for cols, p1 in in_bank:
-                nc.vector.tensor_tensor(out=h[:, cols], in0=p1[:], in1=lev_t[s][:, cols], op=ALU.mult)
+        def scatter(s, cols, values):
+            entries = idx2[:, cols.start // PER_COL : cols.stop // PER_COL]
+            nc.vector.tensor_copy(out=pages[s % PAGES][:].indirect(entries), in_=values[:, cols])
 
-        def place(s, h, th, in_bank):
-            halves = [slice(half * BANK, (half + 1) * BANK) for half in range(S // BANK)]
+        def combine(s, th, y1):
+            h = h_t[s]
+            weighted = ring.tile([P, S], F32, name="weighted", tag="weighted")
             if s == 0:
                 for half, cols in enumerate(halves):
                     engine = nc.vector if half == 0 else nc.gpsimd
                     engine.tensor_tensor(out=h[:, cols], in0=h[:, cols], in1=th[:, cols], op=ALU.add)
-                    engine.tensor_tensor(out=h[:, cols], in0=h[:, cols], in1=wgs_t[:, cols], op=ALU.mult)
-                    entries = idx2[:, half * BANK // PER_COL : (half + 1) * BANK // PER_COL]
-                    nc.vector.tensor_copy(out=page[:].indirect(entries), in_=h[:, cols])
-                return
-            if s == 1:
-                nc.gpsimd.tensor_tensor(out=h[:], in0=h[:], in1=th[:], op=ALU.add)
-            else:
-                first, second = halves
-                nc.gpsimd.tensor_tensor(out=h[:, first], in0=h[:, first], in1=th[:, first], op=ALU.add)
-                nc.gpsimd.tensor_tensor(out=h[:, second], in0=h[:, second], in1=lev_t[s][:, second], op=ALU.mult)
-                nc.gpsimd.tensor_tensor(out=h[:, second], in0=h[:, second], in1=th[:, second], op=ALU.add)
-            nc.gpsimd.tensor_tensor(out=h[:], in0=h[:], in1=wgs_t[:], op=ALU.mult)
-            nc.vector.tensor_copy(out=page[:].indirect(idx2[:]), in_=h[:])
+                    engine.tensor_tensor(out=weighted[:, cols], in0=h[:, cols], in1=wgs_t[:, cols], op=ALU.mult)
+                return weighted
+            cols = slice(max(0, VECTOR_HALVES - 2 * s) * BANK, S)
+            nc.gpsimd.tensor_tensor(out=h[:, cols], in0=h[:, cols], in1=y1[:, cols], op=ALU.mult)
+            nc.gpsimd.tensor_tensor(out=h[:], in0=h[:], in1=th[:], op=ALU.add)
+            nc.gpsimd.tensor_tensor(out=weighted[:], in0=h[:], in1=wgs_t[:], op=ALU.mult)
+            return weighted
 
         z_parts = [
-            [(at, BANK) for at in range(0, M, BANK)],
+            [(0, M)],
             [(starts[c], width) for c, width in enumerate(CHUNKS)],
         ]
         z_bf = [
-            [keep.tile([P, width, PACK], BF16, name="z_bf%d_%d" % (b, at), align_bytes=64) for at, width in z_parts[b]]
-            for b in range(PASSES)
+            [reused.tile([P, M, PACK], BF16, name="z_bf0", offset=0, align_bytes=64)],
+            [keep.tile([P, width, PACK], BF16, name="z_bf1_%d" % at, align_bytes=64) for at, width in z_parts[1]],
         ]
 
-        def pick(s, at, width, tag, bufs):
-            x = ring.tile([P, width], F32, name=tag, tag=tag, bufs=bufs)
+        def pick(s, at, width, x):
             entries = idx3[:, at // PER_COL : (at + width) // PER_COL]
             nc.vector.tensor_tensor(
-                out=x[:], in0=page[:].indirect(entries), in1=mask_t[s][:, at : at + width], op=ALU.add
+                out=x[:], in0=pages[s % PAGES][:].indirect(entries), in1=mask_t[s][:, at : at + width], op=ALU.add
             )
             nc.scalar.activation(out=x[:], in_=x[:], func=ACT.Silu)
             return x
 
-        def gain_and_round(s, part, x):
+        def gain_and_round(s, x, at, width):
             b, i = divmod(s, PACK)
-            nc.scalar.activation(out=z_bf[b][part][:, :, i], in_=x, func=ACT.Copy, scale=gain_t[:, b, i : i + 1])
+            for part, (first, count) in enumerate(z_parts[b]):
+                lo, hi = max(at, first), min(at + width, first + count)
+                if lo < hi:
+                    nc.scalar.activation(
+                        out=z_bf[b][part][:, lo - first : hi - first, i],
+                        in_=x[:, lo - at : hi - at],
+                        func=ACT.Copy,
+                        scale=gain_t[:, b, i : i + 1],
+                    )
+
+        def pick_through_tensor(s, picked):
+            nc.vector.tensor_copy(out=picked[:], in_=pages[s % PAGES][:].indirect(idx3[:]))
+            turned = ring.tile([P, M], F32, name="turned", tag="turned")
+            for half, cols in enumerate(halves):
+                x_t = bank(4 + half, [P, BANK])
+                for at in range(0, BANK, P):
+                    block = slice(half * BANK + at, half * BANK + at + P)
+                    for term, first in ((mask_t[s], True), (picked, False)):
+                        nc.tensor.matmul(
+                            x_t[:, at : at + P], term[:, block], ident[:], start=first, stop=not first, is_transpose=True
+                        )
+                nc.scalar.activation(out=turned[:, cols], in_=x_t[:], func=ACT.Silu)
+            for half, cols in enumerate(halves):
+                back = bank(6 + half, [P, BANK])
+                for at in range(0, BANK, P):
+                    block = slice(half * BANK + at, half * BANK + at + P)
+                    nc.tensor.transpose(back[:, at : at + P], turned[:, block], ident[:])
+                gain_and_round(s, back[:], half * BANK, BANK)
 
         units = [
             (c, first, BANK // width) for c, width in enumerate(CHUNKS) for first in range(0, N // P, BANK // width)
@@ -268,35 +287,50 @@ def tile_list_combiner_intermod_watch_kernel(
         def first_pass(n):
             c, first, per_bank = units[n]
             sums = [bank((2 * n + k) % 8, [P, per_bank, CHUNKS[c]]) for k in range(2)]
-            z_q, z_s = z0[starts[c] // BANK]
-            cols = slice(starts[c] % BANK, starts[c] % BANK + CHUNKS[c])
+            z_q, z_s = z0
+            cols = slice(starts[c], starts[c] + CHUNKS[c])
             score_pass(n, sums, 0, z_q[:, cols], z_s[:, cols])
             return sums
 
-        z0 = []
-        made = [features(0), features(1)]
-        times_lev(0, *made[0])
-        times_lev(1, *made[1])
+        def pick_whole(s):
+            if s in LATE_PICKS:
+                picked = keep.tile([P, M], F32, name="picked%d" % s, tag="h%d" % (s + 1), align_bytes=64)
+            else:
+                picked = ring.tile([P, M], F32, name="picked", tag="picked", bufs=1)
+            if s < FUSED_FROM:
+                pick_through_tensor(s, picked)
+            else:
+                gain_and_round(s, pick(s, 0, M, picked)[:], 0, M)
+
+        made = [features(s) for s in range(PACK)]
         for s in range(SLICES):
+            weighted = combine(s, *made[s])
             if s == SLICES - 1:
+                late_q = keep.tile([P, PASSES * N + M], U32, name="late_q", tag="h%d" % s, align_bytes=64)
+                late_s = keep.tile([P, PASSES * N + M], U8, name="late_s", align_bytes=64)
+                for at, grouped in ((0, w3_bf[:]), (PASSES * N, z_bf[0][0][:].rearrange("p m i -> p (m i)"))):
+                    cols = slice(at, at + M)
+                    nc.vector.quantize_mx(out=late_q[:, cols].bitcast(FP8X4), scales=late_s[:, cols], in_=grouped)
+                w3_mx = [(late_q[:, b * N : (b + 1) * N], late_s[:, b * N : (b + 1) * N]) for b in range(PASSES)]
+                z0 = (late_q[:, PASSES * N :], late_s[:, PASSES * N :])
                 opened = [first_pass(n) for n in range(4)]
-            place(s, *made[s])
-            if s + 2 < SLICES:
-                made.append(features(s + 2))
-            if s + 1 < SLICES:
-                x = pick(s, 0, M, "x", 2)
-                for part, (at, width) in enumerate(z_parts[s // PACK]):
-                    gain_and_round(s, part, x[:, at : at + width])
-            if s + 2 < SLICES:
-                times_lev(s + 2, *made[s + 2])
-            if s == PACK - 1:
-                for part in range(M // BANK):
-                    z0.append(quantise("z0_%d" % part, z_bf[0][part][:].rearrange("p m i -> p (m i)"), BANK))
+            for cols in halves if s == 0 else [slice(0, S)]:
+                scatter(s, cols, weighted)
+            if s == 0:
+                w2_mx.append(quantise("w2_1", round_w2(w2_raw1, "h0")[:], BANK, "w2_1"))
+                made.append(features(PACK))
+            if s + AHEAD < SLICES:
+                made.append(features(s + AHEAD))
+            if s - 1 in LATE_PICKS:
+                pick_whole(s - 1)
+            if s not in LATE_PICKS and s + 1 < SLICES:
+                pick_whole(s)
 
         def last_pick(c):
-            x = pick(SLICES - 1, starts[c], CHUNKS[c], "x_last", len(CHUNKS))
-            gain_and_round(SLICES - 1, c, x[:])
-            return quantise("z1_%d" % c, z_bf[1][c][:].rearrange("p m i -> p (m i)"), CHUNKS[c])
+            x = ring.tile([P, CHUNKS[c]], F32, name="x_last", tag="x_last", bufs=3)
+            pick(SLICES - 1, starts[c], CHUNKS[c], x)
+            gain_and_round(SLICES - 1, x[:], starts[c], CHUNKS[c])
+            return quantise("z1_%d" % c, z_bf[1][c][:].rearrange("p m i -> p (m i)"), CHUNKS[c], "z1_%d" % c)
 
         z1 = [last_pick(0)]
 
@@ -308,9 +342,9 @@ def tile_list_combiner_intermod_watch_kernel(
                 opened.append(first_pass(n))
             sums = opened[n]
             score_pass(n, sums, 1, z1[c][0][:], z1[c][1][:])
-            y2 = ring.tile([P, per_bank, CHUNKS[c]], F32, name="y2", tag="y2")
+            y2 = ring.tile([P, per_bank, CHUNKS[c]], F32, name="y2", tag="y1", bufs=AHEAD)
             nc.scalar.copy(out=y2[:], in_=sums[0][:])
-            y = ring.tile([P, per_bank, CHUNKS[c]], F32, name="y", tag="y", bufs=4)
+            y = ring.tile([P, per_bank, CHUNKS[c]], F32, name="y", tag="th", bufs=AHEAD)
             nc.vector.tensor_tensor(out=y[:], in0=sums[1][:], in1=y2[:], op=ALU.max)
             nc.sync.dma_start(
                 out=out_rows[:, first : first + per_bank, starts[c] : starts[c] + CHUNKS[c]], in_=y[:]

@@ -20,15 +20,19 @@ ALU = mybir.AluOpType
 P = 128
 PACK = 4
 BANK = 512
+BANKS = 8
+QUADRANTS = 4
 PASSES = H // (P * PACK)
 SLICES = PASSES * PACK
 PER_COL = 16
+PAGES = 2
 VECTOR_HALVES = 3
 FUSED_FROM = 5
-PAGES = 2
 LATE_PICKS = range(2, 6)
-AHEAD = 5
+AHEAD = 3
+FEATURE_BUFS = 5
 CHUNKS = (128, 128, 256, 256, 256)
+LAST_PICK_BUFS = 3
 
 
 def tile_list_combiner_intermod_watch_kernel(
@@ -46,9 +50,12 @@ def tile_list_combiner_intermod_watch_kernel(
         def bank(n, shape):
             return psum.tile(shape, F32, name="bank%d" % n, tag="bank%d" % n)
 
-        def load_scale_rows(queue, plane, rows):
-            for q in range(4):
-                queue.dma_start(out=plane[32 * q : 32 * q + 4].bitcast(I32), in_=rows[4 * q : 4 * q + 4].bitcast(I32))
+        def load_scale_rows(queue, scale_tile, rows):
+            for quad in range(QUADRANTS):
+                queue.dma_start(
+                    out=scale_tile[32 * quad : 32 * quad + 4].bitcast(I32),
+                    in_=rows[4 * quad : 4 * quad + 4].bitcast(I32),
+                )
 
         tab_s = keep.tile([P, T], U8, name="tab_s")
         nc.vector.memset(tab_s[:].bitcast(I32), 0)
@@ -90,9 +97,10 @@ def tile_list_combiner_intermod_watch_kernel(
         for page in pages:
             nc.vector.memset(page[:], 0.0)
 
-        for q in range(4):
-            rows = slice(32 * q, 32 * q + 4)
+        for quad in range(QUADRANTS):
+            rows = slice(32 * quad, 32 * quad + 4)
             nc.vector.tensor_copy(out=tab_s[rows].bitcast(I32), in_=tab_s_rows[rows].bitcast(I32))
+
         w1_q = keep.tile([P, 2 * H], U8, name="w1_q", align_bytes=64)
         w1_s = keep.tile([P, H], U8, name="w1_s", align_bytes=64)
         nc.vector.tensor_copy(
@@ -120,21 +128,15 @@ def tile_list_combiner_intermod_watch_kernel(
             )
             return grouped
 
-        def interleave(copy, grouped, planes):
-            copy(
-                out=grouped.rearrange("p (c e i) -> p c i e", e=4, i=PACK),
-                in_=planes.rearrange("p i (c e) -> p c i e", e=4),
-            )
-
         w2_mx = [quantise("w2_0", round_w2(w2_raw0, "w2_bf0")[:], BANK, "w2_0")]
 
         v_q, v_s = [], []
         for half in range(S // BANK):
-            cols = slice(half * BANK // PER_COL, (half + 1) * BANK // PER_COL)
+            entries = idx[:, half * BANK // PER_COL : (half + 1) * BANK // PER_COL]
             v_s.append(keep.tile([P, BANK], U8, name="v_s%d" % half, align_bytes=64))
-            nc.vector.tensor_copy(out=v_s[half][:], in_=tab_s[:].indirect(idx[:, cols]))
+            nc.vector.tensor_copy(out=v_s[half][:], in_=tab_s[:].indirect(entries))
             v_q.append(keep.tile([P, BANK], U32, name="v_q%d" % half, align_bytes=64))
-            nc.vector.tensor_copy(out=v_q[half][:], in_=tab_w[:].bitcast(U32).indirect(idx[:, cols]))
+            nc.vector.tensor_copy(out=v_q[half][:], in_=tab_w[:].bitcast(U32).indirect(entries))
 
         gain_t = keep.tile([P, PASSES, PACK], F32, name="gain_t")
         mask_t = [keep.tile([P, M], F32, name="mask%d" % s) for s in range(SLICES)]
@@ -149,16 +151,19 @@ def tile_list_combiner_intermod_watch_kernel(
                 if s + 2 < SLICES:
                     nc.sync.dma_start(out=h_t[s + 2][:], in_=lev_rows[(s + 2) // PACK, (s + 2) % PACK])
 
-        load_rows(range(0, 3))
+        load_rows(range(0, AHEAD))
         w3_bf = reused.tile([P, PASSES * PACK * N], BF16, name="w3_bf", offset=2 * T, align_bytes=64)
         for b in range(PASSES):
-            interleave(nc.scalar.copy, w3_bf[:, b * PACK * N : (b + 1) * PACK * N], load_weight(w3_rows[b])[:])
+            nc.scalar.copy(
+                out=w3_bf[:, b * PACK * N : (b + 1) * PACK * N].rearrange("p (c e j) -> p c j e", e=4, j=PACK),
+                in_=load_weight(w3_rows[b])[:].rearrange("p j (c e) -> p c j e", e=4),
+            )
         w4_q = keep.tile([P, PASSES, N], I32, name="w4_q", align_bytes=64)
         w4_s = keep.tile([P, PASSES, N], U8, name="w4_s", align_bytes=64)
         nc.gpsimd.memset(w4_s[:].rearrange("p a n -> p (a n)").bitcast(I32), 0)
         nc.sync.dma_start(out=w4_q[:], in_=w4_words.rearrange("a p c i -> p a (c i)").bitcast(I32))
         load_scale_rows(nc.sync, w4_s, w4_scales.rearrange("a r c -> r a c"))
-        load_rows(range(3, SLICES))
+        load_rows(range(AHEAD, SLICES))
         w4_mx = [(w4_q[:, b, :], w4_s[:, b, :]) for b in range(PASSES)]
         starts = [sum(CHUNKS[:c]) for c in range(len(CHUNKS))]
 
@@ -168,8 +173,8 @@ def tile_list_combiner_intermod_watch_kernel(
 
         def features(s):
             b, t = divmod(s, PACK)
-            th = ring.tile([P, S], F32, name="th", tag="th", bufs=AHEAD)
-            y1 = ring.tile([P, S], F32, name="y1", tag="y1", bufs=AHEAD)
+            tanh2 = ring.tile([P, S], F32, name="tanh2", tag="tanh2", bufs=FEATURE_BUFS)
+            prod1 = ring.tile([P, S], F32, name="prod1", tag="prod1", bufs=FEATURE_BUFS)
             for half, cols in enumerate(halves):
                 p2 = bank(2 * half, [P, BANK])
                 p1 = bank(2 * half + 1, [P, BANK])
@@ -191,31 +196,30 @@ def tile_list_combiner_intermod_watch_kernel(
                     start=True,
                     stop=True,
                 )
-                nc.scalar.activation(out=th[:, cols], in_=p2[:], func=ACT.Tanh)
+                nc.scalar.activation(out=tanh2[:, cols], in_=p2[:], func=ACT.Tanh)
                 if 2 * s + half < VECTOR_HALVES:
                     nc.vector.tensor_tensor(out=h_t[s][:, cols], in0=p1[:], in1=h_t[s][:, cols], op=ALU.mult)
                 else:
-                    nc.scalar.copy(out=y1[:, cols], in_=p1[:])
-            return th, y1
+                    nc.scalar.copy(out=prod1[:, cols], in_=p1[:])
+            return tanh2, prod1
+
+        def combine(s, tanh2, prod1):
+            h = h_t[s]
+            weighted = ring.tile([P, S], F32, name="weighted", tag="weighted")
+            if s == 0:
+                for engine, cols in zip((nc.vector, nc.gpsimd), halves):
+                    engine.tensor_tensor(out=h[:, cols], in0=h[:, cols], in1=tanh2[:, cols], op=ALU.add)
+                    engine.tensor_tensor(out=weighted[:, cols], in0=h[:, cols], in1=wgs_t[:, cols], op=ALU.mult)
+                return weighted
+            cols = slice(max(0, VECTOR_HALVES - 2 * s) * BANK, S)
+            nc.gpsimd.tensor_tensor(out=h[:, cols], in0=h[:, cols], in1=prod1[:, cols], op=ALU.mult)
+            nc.gpsimd.tensor_tensor(out=h[:], in0=h[:], in1=tanh2[:], op=ALU.add)
+            nc.gpsimd.tensor_tensor(out=weighted[:], in0=h[:], in1=wgs_t[:], op=ALU.mult)
+            return weighted
 
         def scatter(s, cols, values):
             entries = idx2[:, cols.start // PER_COL : cols.stop // PER_COL]
             nc.vector.tensor_copy(out=pages[s % PAGES][:].indirect(entries), in_=values[:, cols])
-
-        def combine(s, th, y1):
-            h = h_t[s]
-            weighted = ring.tile([P, S], F32, name="weighted", tag="weighted")
-            if s == 0:
-                for half, cols in enumerate(halves):
-                    engine = nc.vector if half == 0 else nc.gpsimd
-                    engine.tensor_tensor(out=h[:, cols], in0=h[:, cols], in1=th[:, cols], op=ALU.add)
-                    engine.tensor_tensor(out=weighted[:, cols], in0=h[:, cols], in1=wgs_t[:, cols], op=ALU.mult)
-                return weighted
-            cols = slice(max(0, VECTOR_HALVES - 2 * s) * BANK, S)
-            nc.gpsimd.tensor_tensor(out=h[:, cols], in0=h[:, cols], in1=y1[:, cols], op=ALU.mult)
-            nc.gpsimd.tensor_tensor(out=h[:], in0=h[:], in1=th[:], op=ALU.add)
-            nc.gpsimd.tensor_tensor(out=weighted[:], in0=h[:], in1=wgs_t[:], op=ALU.mult)
-            return weighted
 
         z_parts = [
             [(0, M)],
@@ -226,71 +230,49 @@ def tile_list_combiner_intermod_watch_kernel(
             [keep.tile([P, width, PACK], BF16, name="z_bf1_%d" % at, align_bytes=64) for at, width in z_parts[1]],
         ]
 
-        def pick(s, at, width, x):
-            entries = idx3[:, at // PER_COL : (at + width) // PER_COL]
-            nc.vector.tensor_tensor(
-                out=x[:], in0=pages[s % PAGES][:].indirect(entries), in1=mask_t[s][:, at : at + width], op=ALU.add
-            )
-            nc.scalar.activation(out=x[:], in_=x[:], func=ACT.Silu)
-            return x
-
         def gain_and_round(s, x, at, width):
             b, i = divmod(s, PACK)
-            for part, (first, count) in enumerate(z_parts[b]):
-                lo, hi = max(at, first), min(at + width, first + count)
+            for part, (part_at, part_width) in enumerate(z_parts[b]):
+                lo, hi = max(at, part_at), min(at + width, part_at + part_width)
                 if lo < hi:
                     nc.scalar.activation(
-                        out=z_bf[b][part][:, lo - first : hi - first, i],
+                        out=z_bf[b][part][:, lo - part_at : hi - part_at, i],
                         in_=x[:, lo - at : hi - at],
                         func=ACT.Copy,
                         scale=gain_t[:, b, i : i + 1],
                     )
 
+        def pick_fused(s, at, width, x):
+            entries = idx3[:, at // PER_COL : (at + width) // PER_COL]
+            nc.vector.tensor_tensor(
+                out=x[:], in0=pages[s % PAGES][:].indirect(entries), in1=mask_t[s][:, at : at + width], op=ALU.add
+            )
+            nc.scalar.activation(out=x[:], in_=x[:], func=ACT.Silu)
+            gain_and_round(s, x[:], at, width)
+
         def pick_through_tensor(s, picked):
             nc.vector.tensor_copy(out=picked[:], in_=pages[s % PAGES][:].indirect(idx3[:]))
             turned = ring.tile([P, M], F32, name="turned", tag="turned")
             for half, cols in enumerate(halves):
-                x_t = bank(4 + half, [P, BANK])
+                x_turned = bank(4 + half, [P, BANK])
                 for at in range(0, BANK, P):
                     block = slice(half * BANK + at, half * BANK + at + P)
-                    for term, first in ((mask_t[s], True), (picked, False)):
+                    for term, opens in ((mask_t[s], True), (picked, False)):
                         nc.tensor.matmul(
-                            x_t[:, at : at + P], term[:, block], ident[:], start=first, stop=not first, is_transpose=True
+                            x_turned[:, at : at + P],
+                            term[:, block],
+                            ident[:],
+                            start=opens,
+                            stop=not opens,
+                            is_transpose=True,
                         )
-                nc.scalar.activation(out=turned[:, cols], in_=x_t[:], func=ACT.Silu)
-            for half, cols in enumerate(halves):
+                nc.scalar.activation(out=turned[:, cols], in_=x_turned[:], func=ACT.Silu)
+            for half in range(M // BANK):
                 back = bank(6 + half, [P, BANK])
                 for at in range(0, BANK, P):
                     block = slice(half * BANK + at, half * BANK + at + P)
                     nc.tensor.transpose(back[:, at : at + P], turned[:, block], ident[:])
                 gain_and_round(s, back[:], half * BANK, BANK)
-
-        units = [
-            (c, first, BANK // width) for c, width in enumerate(CHUNKS) for first in range(0, N // P, BANK // width)
-        ]
-
-        def score_pass(n, sums, b, z_q, z_s):
-            c, first, per_bank = units[n]
-            for acc, weights in zip(sums, (w4_mx, w3_mx)):
-                for g in range(per_bank):
-                    n_cols = slice((first + g) * P, (first + g + 1) * P)
-                    nc.tensor.matmul_mx(
-                        out=acc[:, g, :],
-                        lhsT=weights[b][0][:, n_cols].bitcast(FP8X4),
-                        lhsT_scale=weights[b][1][:, n_cols],
-                        rhs=z_q.bitcast(FP8X4),
-                        rhs_scale=z_s,
-                        start=(b == 0 and g == 0),
-                        stop=(b == PASSES - 1 and g == per_bank - 1),
-                    )
-
-        def first_pass(n):
-            c, first, per_bank = units[n]
-            sums = [bank((2 * n + k) % 8, [P, per_bank, CHUNKS[c]]) for k in range(2)]
-            z_q, z_s = z0
-            cols = slice(starts[c], starts[c] + CHUNKS[c])
-            score_pass(n, sums, 0, z_q[:, cols], z_s[:, cols])
-            return sums
 
         def pick_whole(s):
             if s in LATE_PICKS:
@@ -300,9 +282,34 @@ def tile_list_combiner_intermod_watch_kernel(
             if s < FUSED_FROM:
                 pick_through_tensor(s, picked)
             else:
-                gain_and_round(s, pick(s, 0, M, picked)[:], 0, M)
+                pick_fused(s, 0, M, picked)
 
-        made = [features(s) for s in range(PACK)]
+        units = [
+            (c, tile0, BANK // width) for c, width in enumerate(CHUNKS) for tile0 in range(0, N // P, BANK // width)
+        ]
+
+        def score_pass(n, acc, weights, b, z_q, z_s):
+            c, tile0, tiles = units[n]
+            for g in range(tiles):
+                n_cols = slice((tile0 + g) * P, (tile0 + g + 1) * P)
+                nc.tensor.matmul_mx(
+                    out=acc[:, g, :],
+                    lhsT=weights[b][0][:, n_cols].bitcast(FP8X4),
+                    lhsT_scale=weights[b][1][:, n_cols],
+                    rhs=z_q.bitcast(FP8X4),
+                    rhs_scale=z_s,
+                    start=(b == 0 and g == 0),
+                    stop=(b == PASSES - 1 and g == tiles - 1),
+                )
+
+        def first_pass(n, k):
+            c, tile0, tiles = units[n]
+            acc = bank((2 * n + k) % BANKS, [P, tiles, CHUNKS[c]])
+            cols = slice(starts[c], starts[c] + CHUNKS[c])
+            score_pass(n, acc, score_weights[k], 0, z0_q[:, cols], z0_s[:, cols])
+            return acc
+
+        made = [features(s) for s in range(AHEAD)]
         for s in range(SLICES):
             weighted = combine(s, *made[s])
             if s == SLICES - 1:
@@ -312,13 +319,13 @@ def tile_list_combiner_intermod_watch_kernel(
                     cols = slice(at, at + M)
                     nc.vector.quantize_mx(out=late_q[:, cols].bitcast(FP8X4), scales=late_s[:, cols], in_=grouped)
                 w3_mx = [(late_q[:, b * N : (b + 1) * N], late_s[:, b * N : (b + 1) * N]) for b in range(PASSES)]
-                z0 = (late_q[:, PASSES * N :], late_s[:, PASSES * N :])
-                opened = [first_pass(n) for n in range(4)]
+                z0_q, z0_s = late_q[:, PASSES * N :], late_s[:, PASSES * N :]
+                score_weights = (w4_mx, w3_mx)
+                opened = {(n, k): first_pass(n, k) for n in range(BANKS // 2) for k in range(2)}
             for cols in halves if s == 0 else [slice(0, S)]:
                 scatter(s, cols, weighted)
-            if s == 0:
-                w2_mx.append(quantise("w2_1", round_w2(w2_raw1, "h0")[:], BANK, "w2_1"))
-                made.append(features(PACK))
+            if s + AHEAD == PACK:
+                w2_mx.append(quantise("w2_1", round_w2(w2_raw1, "h0")[:], BANK, "h1"))
             if s + AHEAD < SLICES:
                 made.append(features(s + AHEAD))
             if s - 1 in LATE_PICKS:
@@ -327,25 +334,21 @@ def tile_list_combiner_intermod_watch_kernel(
                 pick_whole(s)
 
         def last_pick(c):
-            x = ring.tile([P, CHUNKS[c]], F32, name="x_last", tag="x_last", bufs=3)
-            pick(SLICES - 1, starts[c], CHUNKS[c], x)
-            gain_and_round(SLICES - 1, x[:], starts[c], CHUNKS[c])
+            x = ring.tile([P, CHUNKS[c]], F32, name="x_last", tag="x_last", bufs=LAST_PICK_BUFS)
+            pick_fused(SLICES - 1, starts[c], CHUNKS[c], x)
             return quantise("z1_%d" % c, z_bf[1][c][:].rearrange("p m i -> p (m i)"), CHUNKS[c], "z1_%d" % c)
 
         z1 = [last_pick(0)]
-
         out_rows = out.rearrange("(t p) m -> p t m", p=P)
-        for n, (c, first, per_bank) in enumerate(units):
-            if first == 0 and c + 1 < len(CHUNKS):
+        for n, (c, tile0, tiles) in enumerate(units):
+            if tile0 == 0 and c + 1 < len(CHUNKS):
                 z1.append(last_pick(c + 1))
-            if n >= len(opened):
-                opened.append(first_pass(n))
-            sums = opened[n]
-            score_pass(n, sums, 1, z1[c][0][:], z1[c][1][:])
-            y2 = ring.tile([P, per_bank, CHUNKS[c]], F32, name="y2", tag="y1", bufs=AHEAD)
-            nc.scalar.copy(out=y2[:], in_=sums[0][:])
-            y = ring.tile([P, per_bank, CHUNKS[c]], F32, name="y", tag="th", bufs=AHEAD)
-            nc.vector.tensor_tensor(out=y[:], in0=sums[1][:], in1=y2[:], op=ALU.max)
-            nc.sync.dma_start(
-                out=out_rows[:, first : first + per_bank, starts[c] : starts[c] + CHUNKS[c]], in_=y[:]
-            )
+            sums = []
+            for k in range(2):
+                sums.append(opened[n, k] if (n, k) in opened else first_pass(n, k))
+                score_pass(n, sums[k], score_weights[k], 1, z1[c][0][:], z1[c][1][:])
+            score4 = ring.tile([P, tiles, CHUNKS[c]], F32, name="score4", tag="prod1", bufs=FEATURE_BUFS)
+            nc.scalar.copy(out=score4[:], in_=sums[0][:])
+            best = ring.tile([P, tiles, CHUNKS[c]], F32, name="best", tag="tanh2", bufs=FEATURE_BUFS)
+            nc.vector.tensor_tensor(out=best[:], in0=sums[1][:], in1=score4[:], op=ALU.max)
+            nc.sync.dma_start(out=out_rows[:, tile0 : tile0 + tiles, starts[c] : starts[c] + CHUNKS[c]], in_=best[:])

from contextlib import ExitStack

import concourse.mybir as mybir
from concourse.masks import make_identity

K, H, N, T, S, T2, M = 512, 1024, 512, 4096, 1024, 2048, 1024
FLOPS = 2 * (2 * K * H * S + 2 * H * N * M)

F32 = mybir.dt.float32
BF16 = mybir.dt.bfloat16
I32 = mybir.dt.int32
U32 = mybir.dt.uint32
U16 = mybir.dt.uint16
U8 = mybir.dt.uint8
FP8X4 = mybir.dt.float8_e4m3fn_x4
FP4X4 = mybir.dt.float4_e2m1fn_x4
ACT = mybir.ActivationFunctionType
ALU = mybir.AluOpType

P = 128
PACK = 4
BANK = 512
BANKS = 8
QUADRANTS = 4
PASSES = H // (P * PACK)
SLICES = PASSES * PACK
PER_COL = 16
PAGES = 2
VECTOR_HALVES = 3
FUSED_FROM = 5
LATE_PICKS = range(2, 6)
AHEAD = 3
FEATURE_BUFS = 5
CHUNKS = (128, 128, 256, 256, 256)
LAST_PICK_BUFS = 3


def tile_list_combiner_intermod_watch_kernel(
    tc, tab_words, tab_scales, offs, w1_words, w1_scales, w2, lev, wgs, offs2, offs3, mask, gain, w3, w4_words,
    w4_scales, out
):
    nc = tc.nc
    with ExitStack() as ctx:
        lists = ctx.enter_context(tc.tile_pool(name="lists", bufs=1))
        keep = ctx.enter_context(tc.tile_pool(name="keep", bufs=1))
        reused = ctx.enter_context(tc.tile_pool(name="reused", bufs=1))
        ring = ctx.enter_context(tc.tile_pool(name="ring", bufs=2))
        psum = ctx.enter_context(tc.psum_pool(name="psum", bufs=1))

        def bank(n, shape):
            return psum.tile(shape, F32, name="bank%d" % n, tag="bank%d" % n)

        def load_scale_rows(queue, scale_tile, rows):
            for quad in range(QUADRANTS):
                queue.dma_start(
                    out=scale_tile[32 * quad : 32 * quad + 4].bitcast(I32),
                    in_=rows[4 * quad : 4 * quad + 4].bitcast(I32),
                )

        tab_s = keep.tile([P, T], U8, name="tab_s")
        nc.vector.memset(tab_s[:].bitcast(I32), 0)
        w1s_raw = keep.tile([P, H], U8, name="w1s_raw")
        nc.gpsimd.memset(w1s_raw[:].bitcast(I32), 0)

        idx = lists.tile([P, S // PER_COL], U16, name="idx")
        idx2 = lists.tile([P, S // PER_COL], U16, name="idx2")
        idx3 = lists.tile([P, M // PER_COL], U16, name="idx3")
        nc.sync.dma_start(idx[:], offs)
        tab_s_rows = ring.tile([P, T], U8, name="tab_s_rows", tag="turned")
        load_scale_rows(nc.sync, tab_s_rows, tab_scales[0])
        load_scale_rows(nc.scalar, w1s_raw, w1_scales[0])
        w1_raw = keep.tile([P, 2 * H], U8, name="w1_raw")
        nc.sync.dma_start(out=w1_raw[:].bitcast(I32), in_=w1_words[0].bitcast(I32))

        w2_rows = w2.rearrange("(p j) c -> p j c", j=PACK)
        w3_rows = w3.rearrange("(b p j) n -> b p j n", b=PASSES, j=PACK)
        lev_rows = lev.rearrange("(b p i) j -> b i p j", b=PASSES, i=PACK)
        mask_rows = mask.rearrange("(b p i) m -> b i p m", b=PASSES, i=PACK)

        def load_weight(rows):
            raw = ring.tile([P, PACK, BANK], F32, name="w_raw", tag="w_raw")
            nc.sync.dma_start(out=raw[:], in_=rows)
            return raw

        w2_raw0 = load_weight(w2_rows[:, :, 0:BANK])
        tab_w = reused.tile([P, T], I32, name="tab_w", offset=0, align_bytes=64)
        nc.sync.dma_start(out=tab_w[:], in_=tab_words[0].rearrange("p t i -> p (t i)").bitcast(I32))
        h_t = [keep.tile([P, S], F32, name="h%d" % s, tag="h%d" % s, align_bytes=64) for s in range(SLICES)]
        wgs_t = keep.tile([P, S], F32, name="wgs_t")
        nc.sync.dma_start(out=h_t[0][:, 0:BANK], in_=lev_rows[0, 0][:, 0:BANK])
        nc.sync.dma_start(out=wgs_t[:, 0:BANK], in_=wgs[:, 0:BANK])
        nc.sync.dma_start(idx2[:], offs2)
        nc.sync.dma_start(out=h_t[0][:, BANK:S], in_=lev_rows[0, 0][:, BANK:S])
        nc.sync.dma_start(out=wgs_t[:, BANK:S], in_=wgs[:, BANK:S])

        pages = [keep.tile([P, T2], F32, name="page%d" % n) for n in range(PAGES)]
        for page in pages:
            nc.vector.memset(page[:], 0.0)

        for quad in range(QUADRANTS):
            rows = slice(32 * quad, 32 * quad + 4)
            nc.vector.tensor_copy(out=tab_s[rows].bitcast(I32), in_=tab_s_rows[rows].bitcast(I32))

        w1_q = keep.tile([P, 2 * H], U8, name="w1_q", align_bytes=64)
        w1_s = keep.tile([P, H], U8, name="w1_s", align_bytes=64)
        nc.vector.tensor_copy(
            out=w1_q[:].bitcast(U16).rearrange("p (b t q) -> p b q t", b=PASSES, t=PACK),
            in_=w1_raw[:].bitcast(U16).rearrange("p (b q t) -> p b q t", b=PASSES, t=PACK),
        )
        for b in range(PASSES):
            cols = slice(b * BANK, (b + 1) * BANK)
            nc.gpsimd.tensor_copy(
                out=w1_s[:, cols].rearrange("p (t q) -> p q t", t=PACK),
                in_=w1s_raw[:, cols].rearrange("p (q t) -> p q t", t=PACK),
            )

        def quantise(name, grouped, width, tag):
            codes = keep.tile([P, width], U32, name=name + "_q", tag=tag, align_bytes=64)
            scales = keep.tile([P, width], U8, name=name + "_s", align_bytes=64)
            nc.vector.quantize_mx(out=codes[:].bitcast(FP8X4), scales=scales[:], in_=grouped)
            return codes, scales

        def round_w2(raw, tag):
            grouped = keep.tile([P, PACK * BANK], BF16, name="w2_bf", tag=tag, align_bytes=64)
            nc.scalar.copy(
                out=grouped[:].rearrange("p (t q j) -> p q j t", t=PACK, j=PACK),
                in_=raw[:].rearrange("p j (q t) -> p q j t", t=PACK),
            )
            return grouped

        w2_mx = [quantise("w2_0", round_w2(w2_raw0, "w2_bf0")[:], BANK, "w2_0")]

        v_q, v_s = [], []
        for half in range(S // BANK):
            entries = idx[:, half * BANK // PER_COL : (half + 1) * BANK // PER_COL]
            v_s.append(keep.tile([P, BANK], U8, name="v_s%d" % half, align_bytes=64))
            nc.vector.tensor_copy(out=v_s[half][:], in_=tab_s[:].indirect(entries))
            v_q.append(keep.tile([P, BANK], U32, name="v_q%d" % half, align_bytes=64))
            nc.vector.tensor_copy(out=v_q[half][:], in_=tab_w[:].bitcast(U32).indirect(entries))

        gain_t = keep.tile([P, PASSES, PACK], F32, name="gain_t")
        mask_t = [keep.tile([P, M], F32, name="mask%d" % s) for s in range(SLICES)]
        nc.sync.dma_start(out=h_t[1][:], in_=lev_rows[0, 1])
        w2_raw1 = load_weight(w2_rows[:, :, BANK:H])
        nc.sync.dma_start(idx3[:], offs3)
        nc.sync.dma_start(out=gain_t[:], in_=gain.rearrange("(b p i) -> p b i", b=PASSES, i=PACK))

        def load_rows(slices):
            for s in slices:
                nc.sync.dma_start(out=mask_t[s][:], in_=mask_rows[s // PACK, s % PACK])
                if s + 2 < SLICES:
                    nc.sync.dma_start(out=h_t[s + 2][:], in_=lev_rows[(s + 2) // PACK, (s + 2) % PACK])

        load_rows(range(0, AHEAD))
        w3_bf = reused.tile([P, PASSES * PACK * N], BF16, name="w3_bf", offset=2 * T, align_bytes=64)
        for b in range(PASSES):
            nc.scalar.copy(
                out=w3_bf[:, b * PACK * N : (b + 1) * PACK * N].rearrange("p (c e j) -> p c j e", e=4, j=PACK),
                in_=load_weight(w3_rows[b])[:].rearrange("p j (c e) -> p c j e", e=4),
            )
        w4_q = keep.tile([P, PASSES, N], I32, name="w4_q", align_bytes=64)
        w4_s = keep.tile([P, PASSES, N], U8, name="w4_s", align_bytes=64)
        nc.gpsimd.memset(w4_s[:].rearrange("p a n -> p (a n)").bitcast(I32), 0)
        nc.sync.dma_start(out=w4_q[:], in_=w4_words.rearrange("a p c i -> p a (c i)").bitcast(I32))
        load_scale_rows(nc.sync, w4_s, w4_scales.rearrange("a r c -> r a c"))
        load_rows(range(AHEAD, SLICES))
        w4_mx = [(w4_q[:, b, :], w4_s[:, b, :]) for b in range(PASSES)]
        starts = [sum(CHUNKS[:c]) for c in range(len(CHUNKS))]

        ident = keep.tile([P, P], F32, name="ident")
        make_identity(nc, ident[:])
        halves = [slice(half * BANK, (half + 1) * BANK) for half in range(S // BANK)]

        def features(s):
            b, t = divmod(s, PACK)
            tanh2 = ring.tile([P, S], F32, name="tanh2", tag="tanh2", bufs=FEATURE_BUFS)
            prod1 = ring.tile([P, S], F32, name="prod1", tag="prod1", bufs=FEATURE_BUFS)
            for half, cols in enumerate(halves):
                p2 = bank(2 * half, [P, BANK])
                p1 = bank(2 * half + 1, [P, BANK])
                nc.tensor.matmul_mx(
                    out=p2[:],
                    lhsT=w2_mx[b][0][:, t * P : (t + 1) * P].bitcast(FP8X4),
                    lhsT_scale=w2_mx[b][1][:, t * P : (t + 1) * P],
                    rhs=v_q[half][:].bitcast(FP8X4),
                    rhs_scale=v_s[half][:],
                    start=True,
                    stop=True,
                )
                nc.tensor.matmul_mx(
                    out=p1[:],
                    lhsT=w1_q[:, 2 * s * P : 2 * (s + 1) * P].bitcast(FP4X4),
                    lhsT_scale=w1_s[:, s * P : (s + 1) * P],
                    rhs=v_q[half][:].bitcast(FP8X4),
                    rhs_scale=v_s[half][:],
                    start=True,
                    stop=True,
                )
                nc.scalar.activation(out=tanh2[:, cols], in_=p2[:], func=ACT.Tanh)
                if 2 * s + half < VECTOR_HALVES:
                    nc.vector.tensor_tensor(out=h_t[s][:, cols], in0=p1[:], in1=h_t[s][:, cols], op=ALU.mult)
                else:
                    nc.scalar.copy(out=prod1[:, cols], in_=p1[:])
            return tanh2, prod1

        def combine(s, tanh2, prod1):
            h = h_t[s]
            weighted = ring.tile([P, S], F32, name="weighted", tag="weighted")
            if s == 0:
                for engine, cols in zip((nc.vector, nc.gpsimd), halves):
                    engine.tensor_tensor(out=h[:, cols], in0=h[:, cols], in1=tanh2[:, cols], op=ALU.add)
                    engine.tensor_tensor(out=weighted[:, cols], in0=h[:, cols], in1=wgs_t[:, cols], op=ALU.mult)
                return weighted
            cols = slice(max(0, VECTOR_HALVES - 2 * s) * BANK, S)
            nc.gpsimd.tensor_tensor(out=h[:, cols], in0=h[:, cols], in1=prod1[:, cols], op=ALU.mult)
            nc.gpsimd.tensor_tensor(out=h[:], in0=h[:], in1=tanh2[:], op=ALU.add)
            nc.gpsimd.tensor_tensor(out=weighted[:], in0=h[:], in1=wgs_t[:], op=ALU.mult)
            return weighted

        def scatter(s, cols, values):
            entries = idx2[:, cols.start // PER_COL : cols.stop // PER_COL]
            nc.vector.tensor_copy(out=pages[s % PAGES][:].indirect(entries), in_=values[:, cols])

        z_parts = [
            [(0, M)],
            [(starts[c], width) for c, width in enumerate(CHUNKS)],
        ]
        z_bf = [
            [reused.tile([P, M, PACK], BF16, name="z_bf0", offset=0, align_bytes=64)],
            [keep.tile([P, width, PACK], BF16, name="z_bf1_%d" % at, align_bytes=64) for at, width in z_parts[1]],
        ]

        def gain_and_round(s, x, at, width):
            b, i = divmod(s, PACK)
            for part, (part_at, part_width) in enumerate(z_parts[b]):
                lo, hi = max(at, part_at), min(at + width, part_at + part_width)
                if lo < hi:
                    nc.scalar.activation(
                        out=z_bf[b][part][:, lo - part_at : hi - part_at, i],
                        in_=x[:, lo - at : hi - at],
                        func=ACT.Copy,
                        scale=gain_t[:, b, i : i + 1],
                    )

        def pick_fused(s, at, width, x):
            entries = idx3[:, at // PER_COL : (at + width) // PER_COL]
            nc.vector.tensor_tensor(
                out=x[:], in0=pages[s % PAGES][:].indirect(entries), in1=mask_t[s][:, at : at + width], op=ALU.add
            )
            nc.scalar.activation(out=x[:], in_=x[:], func=ACT.Silu)
            gain_and_round(s, x[:], at, width)

        def pick_through_tensor(s, picked):
            nc.vector.tensor_copy(out=picked[:], in_=pages[s % PAGES][:].indirect(idx3[:]))
            turned = ring.tile([P, M], F32, name="turned", tag="turned")
            for half, cols in enumerate(halves):
                x_turned = bank(4 + half, [P, BANK])
                for at in range(0, BANK, P):
                    block = slice(half * BANK + at, half * BANK + at + P)
                    for term, opens in ((mask_t[s], True), (picked, False)):
                        nc.tensor.matmul(
                            x_turned[:, at : at + P],
                            term[:, block],
                            ident[:],
                            start=opens,
                            stop=not opens,
                            is_transpose=True,
                        )
                nc.scalar.activation(out=turned[:, cols], in_=x_turned[:], func=ACT.Silu)
            for half in range(M // BANK):
                back = bank(6 + half, [P, BANK])
                for at in range(0, BANK, P):
                    block = slice(half * BANK + at, half * BANK + at + P)
                    nc.tensor.transpose(back[:, at : at + P], turned[:, block], ident[:])
                gain_and_round(s, back[:], half * BANK, BANK)

        def pick_whole(s):
            if s in LATE_PICKS:
                picked = keep.tile([P, M], F32, name="picked%d" % s, tag="h%d" % (s + 1), align_bytes=64)
            else:
                picked = ring.tile([P, M], F32, name="picked", tag="picked", bufs=1)
            if s < FUSED_FROM:
                pick_through_tensor(s, picked)
            else:
                pick_fused(s, 0, M, picked)

        units = [
            (c, tile0, BANK // width) for c, width in enumerate(CHUNKS) for tile0 in range(0, N // P, BANK // width)
        ]

        def score_pass(n, acc, weights, b, z_q, z_s):
            c, tile0, tiles = units[n]
            for g in range(tiles):
                n_cols = slice((tile0 + g) * P, (tile0 + g + 1) * P)
                nc.tensor.matmul_mx(
                    out=acc[:, g, :],
                    lhsT=weights[b][0][:, n_cols].bitcast(FP8X4),
                    lhsT_scale=weights[b][1][:, n_cols],
                    rhs=z_q.bitcast(FP8X4),
                    rhs_scale=z_s,
                    start=(b == 0 and g == 0),
                    stop=(b == PASSES - 1 and g == tiles - 1),
                )

        def first_pass(n, k):
            c, tile0, tiles = units[n]
            acc = bank((2 * n + k) % BANKS, [P, tiles, CHUNKS[c]])
            cols = slice(starts[c], starts[c] + CHUNKS[c])
            score_pass(n, acc, score_weights[k], 0, z0_q[:, cols], z0_s[:, cols])
            return acc

        made = [features(s) for s in range(AHEAD)]
        for s in range(SLICES):
            weighted = combine(s, *made[s])
            if s == SLICES - 1:
                late_q = keep.tile([P, PASSES * N + M], U32, name="late_q", tag="h%d" % s, align_bytes=64)
                late_s = keep.tile([P, PASSES * N + M], U8, name="late_s", align_bytes=64)
                for at, grouped in ((0, w3_bf[:]), (PASSES * N, z_bf[0][0][:].rearrange("p m i -> p (m i)"))):
                    cols = slice(at, at + M)
                    nc.vector.quantize_mx(out=late_q[:, cols].bitcast(FP8X4), scales=late_s[:, cols], in_=grouped)
                w3_mx = [(late_q[:, b * N : (b + 1) * N], late_s[:, b * N : (b + 1) * N]) for b in range(PASSES)]
                z0_q, z0_s = late_q[:, PASSES * N :], late_s[:, PASSES * N :]
                score_weights = (w4_mx, w3_mx)
                opened = {(n, k): first_pass(n, k) for n in range(BANKS // 2) for k in range(2)}
            for cols in halves if s == 0 else [slice(0, S)]:
                scatter(s, cols, weighted)
            if s + AHEAD == PACK:
                w2_mx.append(quantise("w2_1", round_w2(w2_raw1, "h0")[:], BANK, "h1"))
            if s + AHEAD < SLICES:
                made.append(features(s + AHEAD))
            if s - 1 in LATE_PICKS:
                pick_whole(s - 1)
            if s not in LATE_PICKS and s + 1 < SLICES:
                pick_whole(s)

        def last_pick(c):
            x = ring.tile([P, CHUNKS[c]], F32, name="x_last", tag="x_last", bufs=LAST_PICK_BUFS)
            pick_fused(SLICES - 1, starts[c], CHUNKS[c], x)
            return quantise("z1_%d" % c, z_bf[1][c][:].rearrange("p m i -> p (m i)"), CHUNKS[c], "z1_%d" % c)

        z1 = [last_pick(0)]
        out_rows = out.rearrange("(t p) m -> p t m", p=P)
        for n, (c, tile0, tiles) in enumerate(units):
            if tile0 == 0 and c + 1 < len(CHUNKS):
                z1.append(last_pick(c + 1))
            sums = []
            for k in range(2):
                sums.append(opened[n, k] if (n, k) in opened else first_pass(n, k))
                score_pass(n, sums[k], score_weights[k], 1, z1[c][0][:], z1[c][1][:])
            score4 = ring.tile([P, tiles, CHUNKS[c]], F32, name="score4", tag="prod1", bufs=FEATURE_BUFS)
            nc.scalar.copy(out=score4[:], in_=sums[0][:])
            best = ring.tile([P, tiles, CHUNKS[c]], F32, name="best", tag="tanh2", bufs=FEATURE_BUFS)
            nc.vector.tensor_tensor(out=best[:], in0=sums[1][:], in1=score4[:], op=ALU.max)
            nc.sync.dma_start(out=out_rows[:, tile0 : tile0 + tiles, starts[c] : starts[c] + CHUNKS[c]], in_=best[:])
